import numpy as np
import ml_dtypes


def mxq(x, axis, fmt="e4m3"):
    dtype, down = {"e4m3": (ml_dtypes.float8_e4m3fn, 7), "e5m2": (ml_dtypes.float8_e5m2, 14)}[fmt]
    v = np.moveaxis(np.asarray(x, np.float32).astype(ml_dtypes.bfloat16).astype(np.float64), axis, -1)
    blocks = v.reshape(v.shape[:-1] + (-1, 32))
    amax = np.abs(blocks).max(-1, keepdims=True)
    byte = np.maximum(np.where(amax > 0, np.frexp(amax)[1] - 1 + 127, 0) - down, 1)
    scale = np.exp2(byte - 127.0)
    codes = (blocks / scale).astype(np.float32).astype(dtype).astype(np.float64)
    return np.moveaxis((codes * scale).reshape(v.shape), -1, axis)


WIDE = False


def mx_kscale(k):
    if not WIDE:
        return np.ones(k)
    levels = np.array([10, -10, 5, -5, 0])
    if k % 512:
        return np.exp2(np.random.permutation(np.resize(levels, k // 32))).repeat(32)
    a = np.empty((k // 512, 16))
    for p in range(k // 512):
        a[p, :8] = np.random.permutation(np.resize(levels, 8))
        for g in range(8):
            far = levels[np.abs(levels - a[p, g]) >= 10]
            a[p, g + 8] = far[np.random.randint(len(far))]
    return np.exp2(a.ravel()).repeat(32)


def f64(x):
    return np.asarray(x).astype(np.float64)


def striped(idx):
    return np.tile(np.asarray(idx).reshape(-1, 16).T, (8, 1)).astype(np.uint16)


def unstriped(offs):
    return offs[:16].T.reshape(-1).astype(np.int64)


E2M1 = np.array([0.0, 0.5, 1.0, 1.5, 2.0, 3.0, 4.0, 6.0, -0.0, -0.5, -1.0, -1.5, -2.0, -3.0, -4.0, -6.0])


def pack_weight(w, fmt):
    k, n = w.shape
    w = f64(np.asarray(w, np.float32).astype(ml_dtypes.bfloat16)).reshape(k // 32, 32, n)
    amax = np.abs(w).max(1)
    if fmt == "e4m3":
        byte = np.frexp(amax)[1] - 1 + 127 - 7
    else:
        mant, ex = np.frexp(amax / 6.0)
        byte = np.where(mant > 0.5, ex, ex - 1) + 127
    byte = np.clip(np.where(amax > 0, byte, 1), 1, 254)
    scaled = (w * np.exp2(127.0 - byte)[:, None, :]).reshape(k, n).astype(np.float32)
    by_word = np.ascontiguousarray(scaled.reshape(k // 512, 128, 4, n).transpose(0, 1, 3, 2))
    if fmt == "e4m3":
        words = by_word.astype(ml_dtypes.float8_e4m3fn).view(np.uint8)
    else:
        c = by_word.astype(ml_dtypes.float4_e2m1fn).view(np.uint8) & 0xF
        words = (c[..., 0::2] | (c[..., 1::2] << 4)).reshape(k // 512, 128, 2 * n)
    return np.ascontiguousarray(words), np.ascontiguousarray(byte.astype(np.uint8).reshape(k // 512, 16, n))


def unpack_weight(words, scales, fmt):
    g, _, n = scales.shape
    words = np.ascontiguousarray(words).reshape(g, 128, n, -1)
    if fmt == "e4m3":
        vals = words.view(ml_dtypes.float8_e4m3fn).astype(np.float64)
    else:
        nib = np.empty((g, 128, n, 4), np.uint8)
        nib[..., 0::2] = words & 0xF
        nib[..., 1::2] = words >> 4
        vals = E2M1[nib]
    vals = vals * np.repeat(np.exp2(scales.astype(np.float64) - 127.0), 8, axis=1)[..., None]
    return vals.transpose(0, 1, 3, 2).reshape(g * 512, n)


B, N, T, D, NQ = 1, 1024, 4096, 1024, 128
SEG = 64


def setup_inputs():
    n = np.random.standard_normal
    pages = np.random.permutation(T // 64)[:B * N // 64]
    idx = (pages[:, None] * 64 + np.arange(64)[None, :]).reshape(-1)
    s = mx_kscale(D)[:, None]
    kp = pack_weight(n((D, T)) / s, "e2m1")
    return {
        "qT": (n((B, D, NQ)) * s * (1.00 / np.sqrt(D))).astype(np.float32),
        "k_words": np.ascontiguousarray(kp[0].reshape(1, 2, 128, T, 2).transpose(0, 2, 3, 1, 4)).reshape(1, 128, T, 4),
        "k_scales": kp[1],
        "offs": striped(idx),
    }


def reference(qT, k_words, k_scales, offs):
    idx = unstriped(offs)
    pick = lambda x, which: x[:, which].reshape(x.shape[0], B, -1).transpose(1, 0, 2)
    k = unpack_weight(k_words.reshape(1, 128, T, 2, 2).transpose(0, 3, 1, 2, 4).reshape(2, 128, 2 * T), k_scales, "e2m1")
    kg = pick(k, idx)
    qq = mxq(f64(qT), 1, "e4m3")
    a = qq.transpose(0, 2, 1) @ kg
    y = a.reshape(B, NQ, N // SEG, SEG).max(-1) - a.reshape(B, NQ, N // SEG, SEG).mean(-1)
    return y

@@ -1,0 +1,155 @@
+from contextlib import ExitStack
+
+import concourse.mybir as mybir
+
+F32 = mybir.dt.float32
+BF16 = mybir.dt.bfloat16
+I32 = mybir.dt.int32
+U32 = mybir.dt.uint32
+U16 = mybir.dt.uint16
+U8 = mybir.dt.uint8
+FP8X4 = mybir.dt.float8_e4m3fn_x4
+FP4X4 = mybir.dt.float4_e2m1fn_x4
+ALU = mybir.AluOpType
+AX = mybir.AxisListType
+ACT = mybir.ActivationFunctionType
+
+P = 128
+PACK = 4
+PASSES = 2
+T = 4096
+N = 1024
+NQ = 128
+SEG = 64
+HALF = 512
+GROUP = 128
+GROUPS = N // GROUP
+PAGES = N // SEG
+VECTOR_SUM_GROUPS = 2
+FLOPS = 2 * NQ * N * PASSES * P * PACK
+
+
+def tile_attend_pagemean_kernel(tc, qT, k_words, k_scales, offs, out):
+    nc = tc.nc
+    with ExitStack() as ctx:
+        keep = ctx.enter_context(tc.tile_pool(name="keep", bufs=1))
+        psum = ctx.enter_context(tc.psum_pool(name="psum", bufs=1))
+
+        offsets = keep.tile([P, N // 16], U16, name="offsets")
+        scale_pool = keep.tile([P, T], U8, name="scale_pool", align_bytes=64)
+        word_pool = keep.tile([P, T], U32, name="word_pool", align_bytes=64)
+        q_raw = [keep.tile([P, PACK, NQ], F32, name="q_raw%d" % o) for o in range(PASSES)]
+
+        nc.sync.dma_start(offsets[:], offs)
+        nc.sync.dma_start(
+            out=scale_pool[0:32, :].bitcast(I32),
+            in_=k_scales.rearrange("o f t -> (o f) t").bitcast(I32),
+        )
+        nc.sync.dma_start(
+            out=word_pool[:].bitcast(I32),
+            in_=k_words[0].rearrange("p t b -> p (t b)").bitcast(I32),
+        )
+        for o in range(PASSES):
+            rows = qT[0, o * P * PACK : (o + 1) * P * PACK, :]
+            nc.sync.dma_start(out=q_raw[o][:], in_=rows.rearrange("(p j) q -> p j q", j=PACK))
+
+        nc.vector.memset(scale_pool[32:64, :].bitcast(I32), 0)
+        nc.vector.memset(scale_pool[64:128, :].bitcast(I32), 0)
+        k_planes = [keep.tile([P, N], U8, name="k_plane%d" % o, align_bytes=64) for o in range(PASSES)]
+        for o in range(PASSES):
+            nc.vector.memset(k_planes[o][:].bitcast(I32), 0)
+
+        scale_rows = keep.tile([P, N], U8, name="scale_rows", align_bytes=64)
+        nc.vector.tensor_copy(scale_rows[:], scale_pool[:].indirect(offsets[:]))
+        for o in range(PASSES):
+            for quad in range(4):
+                queue = nc.scalar if 4 * o + quad < 5 else nc.gpsimd
+                first = 16 * o + 4 * quad
+                queue.dma_start(
+                    out=k_planes[o][32 * quad : 32 * quad + 4, :].bitcast(I32),
+                    in_=scale_rows[first : first + 4, :].bitcast(I32),
+                )
+
+        q_bf = [keep.tile([P, NQ, PACK], BF16, name="q_bf%d" % o, align_bytes=64) for o in range(PASSES)]
+        q_codes = [keep.tile([P, NQ], U32, name="q_codes%d" % o, align_bytes=64) for o in range(PASSES)]
+        q_planes = [keep.tile([P, NQ], U8, name="q_plane%d" % o, align_bytes=64) for o in range(PASSES)]
+        pairs = [keep.tile([P, HALF], U32, name="pairs%d" % h, align_bytes=64) for h in range(2)]
+        k_codes = [
+            [keep.tile([P, 2 * HALF], U8, name="k_codes%d_%d" % (h, o), align_bytes=64) for o in range(PASSES)]
+            for h in range(2)
+        ]
+        scores = [psum.tile([P, GROUP], F32, name="scores%d" % g) for g in range(GROUPS)]
+
+        def gather(h):
+            cols = HALF // 16
+            nc.vector.tensor_copy(pairs[h][:], word_pool[:].indirect(offsets[:, h * cols : (h + 1) * cols]))
+
+        def part(h, o):
+            halves = pairs[h][:].bitcast(U16).rearrange("p (n o) -> p o n", o=PASSES)
+            nc.vector.tensor_copy(k_codes[h][o][:].bitcast(U16), halves[:, o, :])
+
+        def cast(o):
+            nc.scalar.copy(out=q_bf[o][:], in_=q_raw[o][:].rearrange("p j q -> p q j"))
+
+        def quantize(o):
+            nc.vector.quantize_mx(
+                out=q_codes[o][:].bitcast(FP8X4),
+                scales=q_planes[o][:],
+                in_=q_bf[o][:].rearrange("p q j -> p (q j)"),
+            )
+
+        def multiply(g, o):
+            h, c = divmod(g * GROUP, HALF)
+            nc.tensor.matmul_mx(
+                out=scores[g][:],
+                lhsT=q_codes[o][:].bitcast(FP8X4),
+                lhsT_scale=q_planes[o][:],
+                rhs=k_codes[h][o][:, 2 * c : 2 * (c + GROUP)].bitcast(FP4X4),
+                rhs_scale=k_planes[o][:, g * GROUP : (g + 1) * GROUP],
+                start=(o == 0),
+                stop=(o == PASSES - 1),
+            )
+
+        best = keep.tile([P, PAGES], F32, name="best")
+        total = keep.tile([P, PAGES], F32, name="total")
+        spill = keep.tile([P, PAGES, SEG], F32, name="spill")
+        per = GROUP // SEG
+
+        def reduce_group(g):
+            pages = scores[g][:].rearrange("p (j i) -> p j i", i=SEG)
+            cols = slice(g * per, (g + 1) * per)
+            if g < GROUPS - VECTOR_SUM_GROUPS:
+                for j in range(per):
+                    page = g * per + j
+                    nc.scalar.activation(
+                        out=spill[:, page, :], in_=pages[:, j, :], func=ACT.Copy, accum_out=total[:, page : page + 1]
+                    )
+            else:
+                nc.vector.tensor_reduce(out=total[:, cols], in_=pages, axis=AX.X, op=ALU.add)
+            nc.vector.tensor_reduce(out=best[:, cols], in_=pages, axis=AX.X, op=ALU.max)
+
+        cast(0)
+        cast(1)
+        gather(0)
+        gather(1)
+        part(0, 0)
+        quantize(0)
+        for g in range(4):
+            multiply(g, 0)
+        part(0, 1)
+        part(1, 0)
+        quantize(1)
+        part(1, 1)
+        for g in range(4):
+            multiply(g, 1)
+        for g in range(4, GROUPS):
+            multiply(g, 0)
+            multiply(g, 1)
+        for g in range(GROUPS):
+            reduce_group(g)
+
+        result = keep.tile([P, PAGES], F32, name="result")
+        nc.vector.scalar_tensor_tensor(
+            out=result[:], in0=total[:], scalar=-1.0 / SEG, in1=best[:], op0=ALU.mult, op1=ALU.add
+        )
+        nc.sync.dma_start(out=out[0], in_=result[:])

@@ -53,6 +53,11 @@ def tile_attend_pagemean_kernel(tc, qT, k_words, k_scales, offs, out):
             rows = qT[0, o * P * PACK : (o + 1) * P * PACK, :]
             nc.sync.dma_start(out=q_raw[o][:], in_=rows.rearrange("(p j) q -> p j q", j=PACK))
 
+        one = keep.tile([P, 1], F32, name="one")
+        minus_mean = keep.tile([P, 1], F32, name="minus_mean")
+        nc.vector.memset(one[:], 1.0)
+        nc.scalar.activation(out=minus_mean[:], in_=one[:], func=ACT.Copy, scale=-1.0 / SEG)
+
         nc.vector.memset(scale_pool[32:64, :].bitcast(I32), 0)
         nc.vector.memset(scale_pool[64:128, :].bitcast(I32), 0)
         k_planes = [keep.tile([P, N], U8, name="k_plane%d" % o, align_bytes=64) for o in range(PASSES)]
@@ -61,14 +66,15 @@ def tile_attend_pagemean_kernel(tc, qT, k_words, k_scales, offs, out):
 
         scale_rows = keep.tile([P, N], U8, name="scale_rows", align_bytes=64)
         nc.vector.tensor_copy(scale_rows[:], scale_pool[:].indirect(offsets[:]))
+        nc.vector.tensor_copy(k_planes[0][0:4, :].bitcast(I32), scale_rows[0:4, :].bitcast(I32))
         for o in range(PASSES):
             for quad in range(4):
-                queue = nc.scalar if 4 * o + quad < 5 else nc.gpsimd
                 first = 16 * o + 4 * quad
-                queue.dma_start(
-                    out=k_planes[o][32 * quad : 32 * quad + 4, :].bitcast(I32),
-                    in_=scale_rows[first : first + 4, :].bitcast(I32),
-                )
+                if first > 0:
+                    nc.scalar.dma_start(
+                        out=k_planes[o][32 * quad : 32 * quad + 4, :].bitcast(I32),
+                        in_=scale_rows[first : first + 4, :].bitcast(I32),
+                    )
 
         q_bf = [keep.tile([P, NQ, PACK], BF16, name="q_bf%d" % o, align_bytes=64) for o in range(PASSES)]
         q_codes = [keep.tile([P, NQ], U32, name="q_codes%d" % o, align_bytes=64) for o in range(PASSES)]
@@ -118,6 +124,7 @@ def tile_attend_pagemean_kernel(tc, qT, k_words, k_scales, offs, out):
         def reduce_group(g):
             pages = scores[g][:].rearrange("p (j i) -> p j i", i=SEG)
             cols = slice(g * per, (g + 1) * per)
+            nc.vector.tensor_reduce(out=best[:, cols], in_=pages, axis=AX.X, op=ALU.max)
             if g < GROUPS - VECTOR_SUM_GROUPS:
                 for j in range(per):
                     page = g * per + j
@@ -126,7 +133,6 @@ def tile_attend_pagemean_kernel(tc, qT, k_words, k_scales, offs, out):
                     )
             else:
                 nc.vector.tensor_reduce(out=total[:, cols], in_=pages, axis=AX.X, op=ALU.add)
-            nc.vector.tensor_reduce(out=best[:, cols], in_=pages, axis=AX.X, op=ALU.max)
 
         cast(0)
         cast(1)
@@ -136,20 +142,18 @@ def tile_attend_pagemean_kernel(tc, qT, k_words, k_scales, offs, out):
         quantize(0)
         for g in range(4):
             multiply(g, 0)
-        part(0, 1)
         part(1, 0)
-        quantize(1)
-        part(1, 1)
-        for g in range(4):
-            multiply(g, 1)
         for g in range(4, GROUPS):
             multiply(g, 0)
-            multiply(g, 1)
+        part(0, 1)
+        quantize(1)
+        part(1, 1)
         for g in range(GROUPS):
+            multiply(g, 1)
             reduce_group(g)
 
         result = keep.tile([P, PAGES], F32, name="result")
         nc.vector.scalar_tensor_tensor(
-            out=result[:], in0=total[:], scalar=-1.0 / SEG, in1=best[:], op0=ALU.mult, op1=ALU.add
+            out=result[:], in0=total[:], scalar=minus_mean[:], in1=best[:], op0=ALU.mult, op1=ALU.add
         )
         nc.sync.dma_start(out=out[0], in_=result[:])

@@ -15,17 +15,19 @@ AX = mybir.AxisListType
 ACT = mybir.ActivationFunctionType
 
 P = 128
+QUAD = 32
 PACK = 4
 PASSES = 2
+SCALE_ROWS = 32
 T = 4096
 N = 1024
 NQ = 128
 SEG = 64
-HALF = 512
+PAGES = N // SEG
+HALF = N // 2
 GROUP = 128
 GROUPS = N // GROUP
-PAGES = N // SEG
-VECTOR_SUM_GROUPS = 2
+SCALAR_GROUPS = 5
 FLOPS = 2 * NQ * N * PASSES * P * PACK
 
 
@@ -42,7 +44,7 @@ def tile_attend_pagemean_kernel(tc, qT, k_words, k_scales, offs, out):
 
         nc.sync.dma_start(offsets[:], offs)
         nc.sync.dma_start(
-            out=scale_pool[0:32, :].bitcast(I32),
+            out=scale_pool[0:SCALE_ROWS, :].bitcast(I32),
             in_=k_scales.rearrange("o f t -> (o f) t").bitcast(I32),
         )
         nc.sync.dma_start(
@@ -51,106 +53,117 @@ def tile_attend_pagemean_kernel(tc, qT, k_words, k_scales, offs, out):
         )
         for o in range(PASSES):
             rows = qT[0, o * P * PACK : (o + 1) * P * PACK, :]
-            nc.sync.dma_start(out=q_raw[o][:], in_=rows.rearrange("(p j) q -> p j q", j=PACK))
+            nc.sync.dma_start(out=q_raw[o][:], in_=rows.rearrange("(p t) q -> p t q", t=PACK))
 
         one = keep.tile([P, 1], F32, name="one")
         minus_mean = keep.tile([P, 1], F32, name="minus_mean")
         nc.vector.memset(one[:], 1.0)
         nc.scalar.activation(out=minus_mean[:], in_=one[:], func=ACT.Copy, scale=-1.0 / SEG)
 
-        nc.vector.memset(scale_pool[32:64, :].bitcast(I32), 0)
-        nc.vector.memset(scale_pool[64:128, :].bitcast(I32), 0)
+        nc.vector.memset(scale_pool[QUAD : 2 * QUAD, :].bitcast(I32), 0)
+        nc.vector.memset(scale_pool[2 * QUAD : P, :].bitcast(I32), 0)
+        scale_rows = keep.tile([P, N], U8, name="scale_rows", align_bytes=64)
         k_planes = [keep.tile([P, N], U8, name="k_plane%d" % o, align_bytes=64) for o in range(PASSES)]
         for o in range(PASSES):
-            nc.vector.memset(k_planes[o][:].bitcast(I32), 0)
+            nc.gpsimd.memset(k_planes[o][:].bitcast(I32), 0)
 
-        scale_rows = keep.tile([P, N], U8, name="scale_rows", align_bytes=64)
         nc.vector.tensor_copy(scale_rows[:], scale_pool[:].indirect(offsets[:]))
-        nc.vector.tensor_copy(k_planes[0][0:4, :].bitcast(I32), scale_rows[0:4, :].bitcast(I32))
-        for o in range(PASSES):
-            for quad in range(4):
-                first = 16 * o + 4 * quad
-                if first > 0:
-                    nc.scalar.dma_start(
-                        out=k_planes[o][32 * quad : 32 * quad + 4, :].bitcast(I32),
-                        in_=scale_rows[first : first + 4, :].bitcast(I32),
-                    )
+        nc.vector.tensor_copy(k_planes[0][0:PACK, :].bitcast(I32), scale_rows[0:PACK, :].bitcast(I32))
+        for first in range(PACK, SCALE_ROWS, PACK):
+            o, quad = divmod(first // PACK, P // QUAD)
+            queue = nc.gpsimd if first == SCALE_ROWS - PACK else nc.scalar
+            queue.dma_start(
+                out=k_planes[o][QUAD * quad : QUAD * quad + PACK, :].bitcast(I32),
+                in_=scale_rows[first : first + PACK, :].bitcast(I32),
+            )
 
-        q_bf = [keep.tile([P, NQ, PACK], BF16, name="q_bf%d" % o, align_bytes=64) for o in range(PASSES)]
+        q_bf = [
+            keep.tile([P, NQ, PACK], BF16, name="q_bf%d" % o, tag="stage%d" % o, align_bytes=64) for o in range(PASSES)
+        ]
         q_codes = [keep.tile([P, NQ], U32, name="q_codes%d" % o, align_bytes=64) for o in range(PASSES)]
         q_planes = [keep.tile([P, NQ], U8, name="q_plane%d" % o, align_bytes=64) for o in range(PASSES)]
-        pairs = [keep.tile([P, HALF], U32, name="pairs%d" % h, align_bytes=64) for h in range(2)]
-        k_codes = [
-            [keep.tile([P, 2 * HALF], U8, name="k_codes%d_%d" % (h, o), align_bytes=64) for o in range(PASSES)]
-            for h in range(2)
-        ]
+        pairs = keep.tile([P, N], U32, name="pairs", align_bytes=64)
+        k_codes = {}
+        best = keep.tile([P, PAGES], F32, name="best")
+        total = keep.tile([P, PAGES], F32, name="total")
+        spill = keep.tile([P, PAGES, SEG], F32, name="spill")
         scores = [psum.tile([P, GROUP], F32, name="scores%d" % g) for g in range(GROUPS)]
 
-        def gather(h):
-            cols = HALF // 16
-            nc.vector.tensor_copy(pairs[h][:], word_pool[:].indirect(offsets[:, h * cols : (h + 1) * cols]))
-
-        def part(h, o):
-            halves = pairs[h][:].bitcast(U16).rearrange("p (n o) -> p o n", o=PASSES)
-            nc.vector.tensor_copy(k_codes[h][o][:].bitcast(U16), halves[:, o, :])
-
         def cast(o):
-            nc.scalar.copy(out=q_bf[o][:], in_=q_raw[o][:].rearrange("p j q -> p q j"))
+            nc.scalar.copy(out=q_bf[o][:], in_=q_raw[o][:].rearrange("p t q -> p q t"))
 
         def quantize(o):
             nc.vector.quantize_mx(
                 out=q_codes[o][:].bitcast(FP8X4),
                 scales=q_planes[o][:],
-                in_=q_bf[o][:].rearrange("p q j -> p (q j)"),
+                in_=q_bf[o][:].rearrange("p q t -> p (q t)"),
             )
 
-        def multiply(g, o):
+        def gather(h):
+            a, b = h * HALF, (h + 1) * HALF
+            nc.vector.tensor_copy(pairs[:, a:b], word_pool[:].indirect(offsets[:, a // 16 : b // 16]))
+
+        def part(o, h):
+            words = pairs[:, h * HALF : (h + 1) * HALF].bitcast(U16).rearrange("p (n o) -> p o n", o=PASSES)
+            nc.vector.tensor_copy(k_codes[o, h].bitcast(U16), words[:, o, :])
+
+        def multiply(o, g):
             h, c = divmod(g * GROUP, HALF)
             nc.tensor.matmul_mx(
                 out=scores[g][:],
                 lhsT=q_codes[o][:].bitcast(FP8X4),
                 lhsT_scale=q_planes[o][:],
-                rhs=k_codes[h][o][:, 2 * c : 2 * (c + GROUP)].bitcast(FP4X4),
+                rhs=k_codes[o, h][:, 2 * c : 2 * (c + GROUP)].bitcast(FP4X4),
                 rhs_scale=k_planes[o][:, g * GROUP : (g + 1) * GROUP],
                 start=(o == 0),
                 stop=(o == PASSES - 1),
             )
 
-        best = keep.tile([P, PAGES], F32, name="best")
-        total = keep.tile([P, PAGES], F32, name="total")
-        spill = keep.tile([P, PAGES, SEG], F32, name="spill")
-        per = GROUP // SEG
-
-        def reduce_group(g):
+        def reduce_on_vector(g, into, op):
+            per = GROUP // SEG
             pages = scores[g][:].rearrange("p (j i) -> p j i", i=SEG)
-            cols = slice(g * per, (g + 1) * per)
-            nc.vector.tensor_reduce(out=best[:, cols], in_=pages, axis=AX.X, op=ALU.max)
-            if g < GROUPS - VECTOR_SUM_GROUPS:
-                for j in range(per):
-                    page = g * per + j
-                    nc.scalar.activation(
-                        out=spill[:, page, :], in_=pages[:, j, :], func=ACT.Copy, accum_out=total[:, page : page + 1]
-                    )
-            else:
-                nc.vector.tensor_reduce(out=total[:, cols], in_=pages, axis=AX.X, op=ALU.add)
+            nc.vector.tensor_reduce(out=into[:, g * per : (g + 1) * per], in_=pages, axis=AX.X, op=op)
+
+        def sum_on_scalar(g):
+            for c in range(0, GROUP, SEG):
+                page = (g * GROUP + c) // SEG
+                nc.scalar.activation(
+                    out=spill[:, page, :],
+                    in_=scores[g][:, c : c + SEG],
+                    func=ACT.Copy,
+                    accum_out=total[:, page : page + 1],
+                )
 
         cast(0)
         cast(1)
         gather(0)
         gather(1)
+
+        first_codes = keep.tile([P, 2 * HALF], U8, name="first_codes", align_bytes=64)
+        k_codes[0, 0] = first_codes[:]
         part(0, 0)
         quantize(0)
-        for g in range(4):
-            multiply(g, 0)
-        part(1, 0)
-        for g in range(4, GROUPS):
-            multiply(g, 0)
+        later_codes = keep.tile([P, 3, 2 * HALF], U8, name="later_codes", tag="stage0", align_bytes=64)
+        for slot, key in enumerate([(0, 1), (1, 0), (1, 1)]):
+            k_codes[key] = later_codes[:, slot, :]
+        for g in range(GROUPS // 2):
+            multiply(0, g)
         part(0, 1)
+        for g in range(GROUPS // 2, GROUPS):
+            multiply(0, g)
+        part(1, 0)
         quantize(1)
         part(1, 1)
         for g in range(GROUPS):
-            multiply(g, 1)
-            reduce_group(g)
+            multiply(1, g)
+
+        for g in range(GROUPS):
+            reduce_on_vector(g, best, ALU.max)
+            if g < SCALAR_GROUPS:
+                sum_on_scalar(g)
+            if g > SCALAR_GROUPS:
+                reduce_on_vector(g - 1, total, ALU.add)
+        reduce_on_vector(GROUPS - 1, total, ALU.add)
 
         result = keep.tile([P, PAGES], F32, name="result")
         nc.vector.scalar_tensor_tensor(

@@ -40,12 +40,12 @@ def tile_attend_pagemean_kernel(tc, qT, k_words, k_scales, offs, out):
         offsets = keep.tile([P, N // 16], U16, name="offsets")
         scale_pool = keep.tile([P, T], U8, name="scale_pool", align_bytes=64)
         word_pool = keep.tile([P, T], U32, name="word_pool", align_bytes=64)
-        q_raw = [keep.tile([P, PACK, NQ], F32, name="q_raw%d" % o) for o in range(PASSES)]
+        q_raw = [keep.tile([P, PACK, NQ], F32, name="q_raw%d" % o, tag="raw%d" % o, align_bytes=64) for o in range(PASSES)]
 
         nc.sync.dma_start(offsets[:], offs)
         nc.sync.dma_start(
             out=scale_pool[0:SCALE_ROWS, :].bitcast(I32),
-            in_=k_scales.rearrange("o f t -> (o f) t").bitcast(I32),
+            in_=k_scales.rearrange("o f t -> f o t").bitcast(I32),
         )
         nc.sync.dma_start(
             out=word_pool[:].bitcast(I32),
@@ -63,31 +63,27 @@ def tile_attend_pagemean_kernel(tc, qT, k_words, k_scales, offs, out):
         nc.vector.memset(scale_pool[QUAD : 2 * QUAD, :].bitcast(I32), 0)
         nc.vector.memset(scale_pool[2 * QUAD : P, :].bitcast(I32), 0)
         scale_rows = keep.tile([P, N], U8, name="scale_rows", align_bytes=64)
-        k_planes = [keep.tile([P, N], U8, name="k_plane%d" % o, align_bytes=64) for o in range(PASSES)]
-        for o in range(PASSES):
-            nc.gpsimd.memset(k_planes[o][:].bitcast(I32), 0)
+        k_planes = keep.tile([P, PASSES, N], U8, name="k_planes", align_bytes=64)
+        nc.gpsimd.memset(k_planes[:].bitcast(I32), 0)
 
         nc.vector.tensor_copy(scale_rows[:], scale_pool[:].indirect(offsets[:]))
-        nc.vector.tensor_copy(k_planes[0][0:PACK, :].bitcast(I32), scale_rows[0:PACK, :].bitcast(I32))
-        for first in range(PACK, SCALE_ROWS, PACK):
-            o, quad = divmod(first // PACK, P // QUAD)
-            queue = nc.gpsimd if first == SCALE_ROWS - PACK else nc.scalar
-            queue.dma_start(
-                out=k_planes[o][QUAD * quad : QUAD * quad + PACK, :].bitcast(I32),
-                in_=scale_rows[first : first + PACK, :].bitcast(I32),
+        for quad in range(P // QUAD):
+            first = quad * PACK * PASSES
+            nc.scalar.dma_start(
+                out=k_planes[QUAD * quad : QUAD * quad + PACK, :, :].bitcast(I32),
+                in_=scale_rows[first : first + PACK * PASSES, :].bitcast(I32),
             )
 
         q_bf = [
-            keep.tile([P, NQ, PACK], BF16, name="q_bf%d" % o, tag="stage%d" % o, align_bytes=64) for o in range(PASSES)
+            keep.tile([P, NQ, PACK], BF16, name="q_bf%d" % o, align_bytes=64) for o in range(PASSES)
         ]
         q_codes = [keep.tile([P, NQ], U32, name="q_codes%d" % o, align_bytes=64) for o in range(PASSES)]
         q_planes = [keep.tile([P, NQ], U8, name="q_plane%d" % o, align_bytes=64) for o in range(PASSES)]
-        pairs = keep.tile([P, N], U32, name="pairs", align_bytes=64)
-        k_codes = {}
         best = keep.tile([P, PAGES], F32, name="best")
         total = keep.tile([P, PAGES], F32, name="total")
         spill = keep.tile([P, PAGES, SEG], F32, name="spill")
-        scores = [psum.tile([P, GROUP], F32, name="scores%d" % g) for g in range(GROUPS)]
+        spans = [(first, GROUP) for first in range(0, N, GROUP)]
+        scores = [psum.tile([P, width], F32, name="scores%d" % b) for b, (first, width) in enumerate(spans)]
 
         def cast(o):
             nc.scalar.copy(out=q_bf[o][:], in_=q_raw[o][:].rearrange("p t q -> p q t"))
@@ -99,71 +95,67 @@ def tile_attend_pagemean_kernel(tc, qT, k_words, k_scales, offs, out):
                 in_=q_bf[o][:].rearrange("p q t -> p (q t)"),
             )
 
-        def gather(h):
+        def gather(h, pairs):
             a, b = h * HALF, (h + 1) * HALF
-            nc.vector.tensor_copy(pairs[:, a:b], word_pool[:].indirect(offsets[:, a // 16 : b // 16]))
+            nc.vector.tensor_copy(pairs, word_pool[:].indirect(offsets[:, a // 16 : b // 16]))
 
-        def part(o, h):
-            words = pairs[:, h * HALF : (h + 1) * HALF].bitcast(U16).rearrange("p (n o) -> p o n", o=PASSES)
-            nc.vector.tensor_copy(k_codes[o, h].bitcast(U16), words[:, o, :])
+        def halves(pairs):
+            return pairs.bitcast(U16).rearrange("p (n o) -> p o n", o=PASSES)
 
-        def multiply(o, g):
-            h, c = divmod(g * GROUP, HALF)
+        def multiply(o, b, at, width, words):
+            slot = spans[b][0] + at
             nc.tensor.matmul_mx(
-                out=scores[g][:],
+                out=scores[b][:, at : at + width],
                 lhsT=q_codes[o][:].bitcast(FP8X4),
                 lhsT_scale=q_planes[o][:],
-                rhs=k_codes[o, h][:, 2 * c : 2 * (c + GROUP)].bitcast(FP4X4),
-                rhs_scale=k_planes[o][:, g * GROUP : (g + 1) * GROUP],
+                rhs=words.bitcast(FP4X4),
+                rhs_scale=k_planes[:, o, slot : slot + width],
                 start=(o == 0),
                 stop=(o == PASSES - 1),
             )
 
-        def reduce_on_vector(g, into, op):
-            per = GROUP // SEG
-            pages = scores[g][:].rearrange("p (j i) -> p j i", i=SEG)
-            nc.vector.tensor_reduce(out=into[:, g * per : (g + 1) * per], in_=pages, axis=AX.X, op=op)
+        def reduce_on_vector(b, into, op):
+            first, width = spans[b]
+            pages = scores[b][:].rearrange("p (j i) -> p j i", i=SEG)
+            nc.vector.tensor_reduce(out=into[:, first // SEG : (first + width) // SEG], in_=pages, axis=AX.X, op=op)
 
-        def sum_on_scalar(g):
-            for c in range(0, GROUP, SEG):
-                page = (g * GROUP + c) // SEG
+        def sum_on_scalar(b):
+            first, width = spans[b]
+            for c in range(0, width, SEG):
+                page = (first + c) // SEG
                 nc.scalar.activation(
                     out=spill[:, page, :],
-                    in_=scores[g][:, c : c + SEG],
+                    in_=scores[b][:, c : c + SEG],
                     func=ACT.Copy,
                     accum_out=total[:, page : page + 1],
                 )
 
         cast(0)
         cast(1)
-        gather(0)
-        gather(1)
-
-        first_codes = keep.tile([P, 2 * HALF], U8, name="first_codes", align_bytes=64)
-        k_codes[0, 0] = first_codes[:]
-        part(0, 0)
+        pairs = [keep.tile([P, HALF], U32, name="pairs%d" % h, align_bytes=64) for h in range(2)]
+        gather(0, pairs[0][:])
+        gather(1, pairs[1][:])
+        codes00 = keep.tile([P, 2 * HALF], U8, name="codes00", align_bytes=64)
+        nc.vector.tensor_copy(codes00[:].bitcast(U16), halves(pairs[0][:])[:, 0, :])
         quantize(0)
-        later_codes = keep.tile([P, 3, 2 * HALF], U8, name="later_codes", tag="stage0", align_bytes=64)
-        for slot, key in enumerate([(0, 1), (1, 0), (1, 1)]):
-            k_codes[key] = later_codes[:, slot, :]
-        for g in range(GROUPS // 2):
-            multiply(0, g)
-        part(0, 1)
-        for g in range(GROUPS // 2, GROUPS):
-            multiply(0, g)
-        part(1, 0)
+        codes10 = keep.tile([P, 2 * HALF], U8, name="codes10", tag="raw0", align_bytes=64)
+        nc.vector.tensor_copy(codes10[:].bitcast(U16), halves(pairs[0][:])[:, 1, :])
         quantize(1)
-        part(1, 1)
-        for g in range(GROUPS):
-            multiply(1, g)
-
-        for g in range(GROUPS):
+        for o, codes in enumerate([codes00, codes10]):
+            for g in range(GROUPS // 2):
+                multiply(o, g, 0, GROUP, codes[:, 2 * g * GROUP : 2 * (g + 1) * GROUP])
+        later = keep.tile([P, PASSES, 2 * HALF], U8, name="later", tag="raw1", align_bytes=64)
+        nc.vector.tensor_copy(later[:].bitcast(U16), halves(pairs[1][:]))
+        for g in range(GROUPS // 2):
+            for o in range(PASSES):
+                multiply(o, GROUPS // 2 + g, 0, GROUP, later[:, o, 2 * g * GROUP : 2 * (g + 1) * GROUP])
+        sum_on_scalar(0)
+        sum_on_scalar(1)
+        for g in [2, 3, 0, 1, 4, 5, 6, 7]:
             reduce_on_vector(g, best, ALU.max)
-            if g < SCALAR_GROUPS:
+            if 1 < g < 7:
                 sum_on_scalar(g)
-            if g > SCALAR_GROUPS:
-                reduce_on_vector(g - 1, total, ALU.add)
-        reduce_on_vector(GROUPS - 1, total, ALU.add)
+        reduce_on_vector(7, total, ALU.add)
 
         result = keep.tile([P, PAGES], F32, name="result")
         nc.vector.scalar_tensor_tensor(

@@ -83,10 +83,14 @@ def tile_attend_pagemean_kernel(tc, qT, k_words, k_scales, offs, out):
         total = keep.tile([P, PAGES], F32, name="total")
         spill = keep.tile([P, PAGES, SEG], F32, name="spill")
         spans = [(first, GROUP) for first in range(0, N, GROUP)]
-        scores = [psum.tile([P, width], F32, name="scores%d" % b) for b, (first, width) in enumerate(spans)]
+        banks = [psum.tile([P, HALF], F32, name="bank%d" % b) for b in range(GROUPS)]
+        scores = [bank[:, 0:GROUP] for bank in banks]
 
         def cast(o):
-            nc.scalar.copy(out=q_bf[o][:], in_=q_raw[o][:].rearrange("p t q -> p q t"))
+            nc.scalar.copy(
+                out=q_bf[o][:].rearrange("p (c i) t -> p c t i", i=PACK),
+                in_=q_raw[o][:].rearrange("p t (c i) -> p c t i", i=PACK),
+            )
 
         def quantize(o):
             nc.vector.quantize_mx(
@@ -116,7 +120,7 @@ def tile_attend_pagemean_kernel(tc, qT, k_words, k_scales, offs, out):
 
         def reduce_on_vector(b, into, op):
             first, width = spans[b]
-            pages = scores[b][:].rearrange("p (j i) -> p j i", i=SEG)
+            pages = scores[b].rearrange("p (j i) -> p j i", i=SEG)
             nc.vector.tensor_reduce(out=into[:, first // SEG : (first + width) // SEG], in_=pages, axis=AX.X, op=op)
 
         def sum_on_scalar(b):
@@ -134,6 +138,20 @@ def tile_attend_pagemean_kernel(tc, qT, k_words, k_scales, offs, out):
         cast(1)
         pairs = [keep.tile([P, HALF], U32, name="pairs%d" % h, align_bytes=64) for h in range(2)]
         gather(0, pairs[0][:])
+        warm_in = keep.tile([P, PACK * P], BF16, name="warm_in", align_bytes=64)
+        warm_codes = keep.tile([P, P], U32, name="warm_codes", align_bytes=64)
+        warm_plane = keep.tile([P, P], U8, name="warm_plane", align_bytes=64)
+        nc.vector.memset(warm_in[:], 1.0)
+        nc.vector.quantize_mx(out=warm_codes[:].bitcast(FP8X4), scales=warm_plane[:], in_=warm_in[:])
+        nc.tensor.matmul_mx(
+            out=banks[GROUPS - 1][:],
+            lhsT=warm_codes[:].bitcast(FP8X4),
+            lhsT_scale=warm_plane[:],
+            rhs=pairs[0][:, HALF // 2 : HALF].bitcast(FP4X4),
+            rhs_scale=scale_rows[:, 0:HALF],
+            start=True,
+            stop=True,
+        )
         gather(1, pairs[1][:])
         codes00 = keep.tile([P, 2 * HALF], U8, name="codes00", align_bytes=64)
         nc.vector.tensor_copy(codes00[:].bitcast(U16), halves(pairs[0][:])[:, 0, :])

@@ -138,20 +138,6 @@ def tile_attend_pagemean_kernel(tc, qT, k_words, k_scales, offs, out):
         cast(1)
         pairs = [keep.tile([P, HALF], U32, name="pairs%d" % h, align_bytes=64) for h in range(2)]
         gather(0, pairs[0][:])
-        warm_in = keep.tile([P, PACK * P], BF16, name="warm_in", align_bytes=64)
-        warm_codes = keep.tile([P, P], U32, name="warm_codes", align_bytes=64)
-        warm_plane = keep.tile([P, P], U8, name="warm_plane", align_bytes=64)
-        nc.vector.memset(warm_in[:], 1.0)
-        nc.vector.quantize_mx(out=warm_codes[:].bitcast(FP8X4), scales=warm_plane[:], in_=warm_in[:])
-        nc.tensor.matmul_mx(
-            out=banks[GROUPS - 1][:],
-            lhsT=warm_codes[:].bitcast(FP8X4),
-            lhsT_scale=warm_plane[:],
-            rhs=pairs[0][:, HALF // 2 : HALF].bitcast(FP4X4),
-            rhs_scale=scale_rows[:, 0:HALF],
-            start=True,
-            stop=True,
-        )
         gather(1, pairs[1][:])
         codes00 = keep.tile([P, 2 * HALF], U8, name="codes00", align_bytes=64)
         nc.vector.tensor_copy(codes00[:].bitcast(U16), halves(pairs[0][:])[:, 0, :])

@@ -19,6 +19,7 @@ QUAD = 32
 PACK = 4
 PASSES = 2
 SCALE_ROWS = 32
+ROW_STEP = P // SCALE_ROWS
 T = 4096
 N = 1024
 NQ = 128
@@ -27,7 +28,8 @@ PAGES = N // SEG
 HALF = N // 2
 GROUP = 128
 GROUPS = N // GROUP
-SCALAR_GROUPS = 5
+PIECE = 2 * GROUP
+SCALAR_FIRST = 4
 FLOPS = 2 * NQ * N * PASSES * P * PACK
 
 
@@ -39,57 +41,48 @@ def tile_attend_pagemean_kernel(tc, qT, k_words, k_scales, offs, out):
 
         offsets = keep.tile([P, N // 16], U16, name="offsets")
         scale_pool = keep.tile([P, T], U8, name="scale_pool", align_bytes=64)
-        word_pool = keep.tile([P, T], U32, name="word_pool", align_bytes=64)
-        q_raw = [keep.tile([P, PACK, NQ], F32, name="q_raw%d" % o, tag="raw%d" % o, align_bytes=64) for o in range(PASSES)]
+
+        def load_queries(o):
+            raw = keep.tile([P, PACK, NQ], F32, name="q_raw%d" % o, tag="raw", align_bytes=64)
+            rows = qT[0, o * P * PACK : (o + 1) * P * PACK, :]
+            nc.sync.dma_start(out=raw[:], in_=rows.rearrange("(p t) q -> p t q", t=PACK))
+            return raw
+
+        one = keep.tile([P, 1], F32, name="one", tag="words", align_bytes=64)
+        minus_mean = keep.tile([P, 1], F32, name="minus_mean")
+        nc.vector.memset(one[:], 1.0)
+        nc.vector.memset(scale_pool[:].bitcast(I32), 0)
+        nc.vector.tensor_scalar_mul(minus_mean[:], one[:], -1.0 / SEG)
 
         nc.sync.dma_start(offsets[:], offs)
+        q_raw0 = load_queries(0)
         nc.sync.dma_start(
-            out=scale_pool[0:SCALE_ROWS, :].bitcast(I32),
+            out=scale_pool[0:P:ROW_STEP, :].bitcast(I32),
             in_=k_scales.rearrange("o f t -> f o t").bitcast(I32),
         )
+        word_pool = keep.tile([P, T], U32, name="word_pool", tag="words", align_bytes=64)
         nc.sync.dma_start(
             out=word_pool[:].bitcast(I32),
             in_=k_words[0].rearrange("p t b -> p (t b)").bitcast(I32),
         )
-        for o in range(PASSES):
-            rows = qT[0, o * P * PACK : (o + 1) * P * PACK, :]
-            nc.sync.dma_start(out=q_raw[o][:], in_=rows.rearrange("(p t) q -> p t q", t=PACK))
 
-        one = keep.tile([P, 1], F32, name="one")
-        minus_mean = keep.tile([P, 1], F32, name="minus_mean")
-        nc.vector.memset(one[:], 1.0)
-        nc.scalar.activation(out=minus_mean[:], in_=one[:], func=ACT.Copy, scale=-1.0 / SEG)
-
-        nc.vector.memset(scale_pool[QUAD : 2 * QUAD, :].bitcast(I32), 0)
-        nc.vector.memset(scale_pool[2 * QUAD : P, :].bitcast(I32), 0)
         scale_rows = keep.tile([P, N], U8, name="scale_rows", align_bytes=64)
         k_planes = keep.tile([P, PASSES, N], U8, name="k_planes", align_bytes=64)
-        nc.gpsimd.memset(k_planes[:].bitcast(I32), 0)
+        nc.vector.memset(k_planes[:].bitcast(I32), 0)
 
-        nc.vector.tensor_copy(scale_rows[:], scale_pool[:].indirect(offsets[:]))
-        for quad in range(P // QUAD):
-            first = quad * PACK * PASSES
-            nc.scalar.dma_start(
-                out=k_planes[QUAD * quad : QUAD * quad + PACK, :, :].bitcast(I32),
-                in_=scale_rows[first : first + PACK * PASSES, :].bitcast(I32),
-            )
-
-        q_bf = [
-            keep.tile([P, NQ, PACK], BF16, name="q_bf%d" % o, align_bytes=64) for o in range(PASSES)
-        ]
+        q_bf = [keep.tile([P, NQ, PACK], BF16, name="q_bf%d" % o, align_bytes=64) for o in range(PASSES)]
         q_codes = [keep.tile([P, NQ], U32, name="q_codes%d" % o, align_bytes=64) for o in range(PASSES)]
         q_planes = [keep.tile([P, NQ], U8, name="q_plane%d" % o, align_bytes=64) for o in range(PASSES)]
         best = keep.tile([P, PAGES], F32, name="best")
         total = keep.tile([P, PAGES], F32, name="total")
         spill = keep.tile([P, PAGES, SEG], F32, name="spill")
-        spans = [(first, GROUP) for first in range(0, N, GROUP)]
         banks = [psum.tile([P, HALF], F32, name="bank%d" % b) for b in range(GROUPS)]
         scores = [bank[:, 0:GROUP] for bank in banks]
 
-        def cast(o):
+        def cast(o, raw):
             nc.scalar.copy(
                 out=q_bf[o][:].rearrange("p (c i) t -> p c t i", i=PACK),
-                in_=q_raw[o][:].rearrange("p t (c i) -> p c t i", i=PACK),
+                in_=raw[:].rearrange("p t (c i) -> p c t i", i=PACK),
             )
 
         def quantize(o):
@@ -106,60 +99,69 @@ def tile_attend_pagemean_kernel(tc, qT, k_words, k_scales, offs, out):
         def halves(pairs):
             return pairs.bitcast(U16).rearrange("p (n o) -> p o n", o=PASSES)
 
-        def multiply(o, b, at, width, words):
-            slot = spans[b][0] + at
+        def multiply(o, g, words):
             nc.tensor.matmul_mx(
-                out=scores[b][:, at : at + width],
+                out=scores[g],
                 lhsT=q_codes[o][:].bitcast(FP8X4),
                 lhsT_scale=q_planes[o][:],
                 rhs=words.bitcast(FP4X4),
-                rhs_scale=k_planes[:, o, slot : slot + width],
+                rhs_scale=k_planes[:, o, g * GROUP : (g + 1) * GROUP],
                 start=(o == 0),
                 stop=(o == PASSES - 1),
             )
 
-        def reduce_on_vector(b, into, op):
-            first, width = spans[b]
-            pages = scores[b].rearrange("p (j i) -> p j i", i=SEG)
-            nc.vector.tensor_reduce(out=into[:, first // SEG : (first + width) // SEG], in_=pages, axis=AX.X, op=op)
+        def reduce_on_vector(g, into, op):
+            pages = scores[g].rearrange("p (j i) -> p j i", i=SEG)
+            first = g * GROUP // SEG
+            nc.vector.tensor_reduce(out=into[:, first : first + GROUP // SEG], in_=pages, axis=AX.X, op=op)
 
-        def sum_on_scalar(b):
-            first, width = spans[b]
-            for c in range(0, width, SEG):
-                page = (first + c) // SEG
+        def sum_on_scalar(g):
+            for c in range(0, GROUP, SEG):
+                page = (g * GROUP + c) // SEG
                 nc.scalar.activation(
                     out=spill[:, page, :],
-                    in_=scores[b][:, c : c + SEG],
+                    in_=scores[g][:, c : c + SEG],
                     func=ACT.Copy,
                     accum_out=total[:, page : page + 1],
                 )
 
-        cast(0)
-        cast(1)
-        pairs = [keep.tile([P, HALF], U32, name="pairs%d" % h, align_bytes=64) for h in range(2)]
-        gather(0, pairs[0][:])
-        gather(1, pairs[1][:])
-        codes00 = keep.tile([P, 2 * HALF], U8, name="codes00", align_bytes=64)
-        nc.vector.tensor_copy(codes00[:].bitcast(U16), halves(pairs[0][:])[:, 0, :])
+        cast(0, q_raw0)
+        q_raw1 = load_queries(1)
+        nc.vector.tensor_copy(scale_rows[:], scale_pool[:].indirect(offsets[:]))
         quantize(0)
-        codes10 = keep.tile([P, 2 * HALF], U8, name="codes10", tag="raw0", align_bytes=64)
-        nc.vector.tensor_copy(codes10[:].bitcast(U16), halves(pairs[0][:])[:, 1, :])
-        quantize(1)
-        for o, codes in enumerate([codes00, codes10]):
-            for g in range(GROUPS // 2):
-                multiply(o, g, 0, GROUP, codes[:, 2 * g * GROUP : 2 * (g + 1) * GROUP])
-        later = keep.tile([P, PASSES, 2 * HALF], U8, name="later", tag="raw1", align_bytes=64)
-        nc.vector.tensor_copy(later[:].bitcast(U16), halves(pairs[1][:]))
-        for g in range(GROUPS // 2):
-            for o in range(PASSES):
-                multiply(o, GROUPS // 2 + g, 0, GROUP, later[:, o, 2 * g * GROUP : 2 * (g + 1) * GROUP])
-        sum_on_scalar(0)
-        sum_on_scalar(1)
-        for g in [2, 3, 0, 1, 4, 5, 6, 7]:
+        for quad in (0, 2, 1, 3):
+            nc.scalar.dma_start(
+                out=k_planes[QUAD * quad : QUAD * quad + PACK, :, :].bitcast(I32),
+                in_=scale_rows[QUAD * quad : QUAD * (quad + 1) : ROW_STEP, :].bitcast(I32),
+            )
+        cast(1, q_raw1)
+
+        pairs = keep.tile([P, N], U32, name="pairs", align_bytes=64)
+        gather(0, pairs[:, 0:HALF])
+        gather(1, pairs[:, HALF:N])
+        for o in range(PASSES):
+            codes = keep.tile([P, 2 * PIECE], U8, name="first%d" % o, align_bytes=64)
+            nc.vector.tensor_copy(codes[:].bitcast(U16), halves(pairs[:, 0:PIECE])[:, o, :])
+            if o == 1:
+                quantize(1)
+            for g in range(PIECE // GROUP):
+                multiply(o, g, codes[:, 2 * g * GROUP : 2 * (g + 1) * GROUP])
+        later = keep.tile([P, N // PIECE - 1, PASSES, 2 * PIECE], U8, name="later", tag="raw", align_bytes=64)
+        for piece in range(1, N // PIECE):
+            nc.vector.tensor_copy(
+                later[:, piece - 1].bitcast(U16), halves(pairs[:, piece * PIECE : (piece + 1) * PIECE])
+            )
+            for at in range(0, PIECE, GROUP):
+                for o in range(PASSES):
+                    multiply(o, (piece * PIECE + at) // GROUP, later[:, piece - 1, o, 2 * at : 2 * (at + GROUP)])
+        for g in range(SCALAR_FIRST):
+            sum_on_scalar(g)
+        for g in range(GROUPS):
             reduce_on_vector(g, best, ALU.max)
-            if 1 < g < 7:
+            if SCALAR_FIRST <= g < GROUPS - 1:
                 sum_on_scalar(g)
-        reduce_on_vector(7, total, ALU.add)
+        reduce_on_vector(GROUPS - 1, total, ALU.add)
+
 
         result = keep.tile([P, PAGES], F32, name="result")
         nc.vector.scalar_tensor_tensor(

@@ -19,7 +19,7 @@ QUAD = 32
 PACK = 4
 PASSES = 2
 SCALE_ROWS = 32
-ROW_STEP = P // SCALE_ROWS
+FIRST_ROW = P - SCALE_ROWS
 T = 4096
 N = 1024
 NQ = 128
@@ -48,23 +48,19 @@ def tile_attend_pagemean_kernel(tc, qT, k_words, k_scales, offs, out):
             nc.sync.dma_start(out=raw[:], in_=rows.rearrange("(p t) q -> p t q", t=PACK))
             return raw
 
-        one = keep.tile([P, 1], F32, name="one", tag="words", align_bytes=64)
-        minus_mean = keep.tile([P, 1], F32, name="minus_mean")
-        nc.vector.memset(one[:], 1.0)
-        nc.vector.memset(scale_pool[:].bitcast(I32), 0)
-        nc.vector.tensor_scalar_mul(minus_mean[:], one[:], -1.0 / SEG)
-
-        nc.sync.dma_start(offsets[:], offs)
-        q_raw0 = load_queries(0)
+        word_pool = keep.tile([P, T], U32, name="word_pool", align_bytes=64)
         nc.sync.dma_start(
-            out=scale_pool[0:P:ROW_STEP, :].bitcast(I32),
+            out=scale_pool[FIRST_ROW:P, :].bitcast(I32),
             in_=k_scales.rearrange("o f t -> f o t").bitcast(I32),
         )
-        word_pool = keep.tile([P, T], U32, name="word_pool", tag="words", align_bytes=64)
+        nc.sync.dma_start(offsets[:], offs)
+        q_raw0 = load_queries(0)
         nc.sync.dma_start(
             out=word_pool[:].bitcast(I32),
             in_=k_words[0].rearrange("p t b -> p (t b)").bitcast(I32),
         )
+
+        nc.vector.memset(scale_pool[0:FIRST_ROW, :].bitcast(I32), 0)
 
         scale_rows = keep.tile([P, N], U8, name="scale_rows", align_bytes=64)
         k_planes = keep.tile([P, PASSES, N], U8, name="k_planes", align_bytes=64)
@@ -129,10 +125,11 @@ def tile_attend_pagemean_kernel(tc, qT, k_words, k_scales, offs, out):
         q_raw1 = load_queries(1)
         nc.vector.tensor_copy(scale_rows[:], scale_pool[:].indirect(offsets[:]))
         quantize(0)
+        rows = PACK * PASSES
         for quad in (0, 2, 1, 3):
             nc.scalar.dma_start(
                 out=k_planes[QUAD * quad : QUAD * quad + PACK, :, :].bitcast(I32),
-                in_=scale_rows[QUAD * quad : QUAD * (quad + 1) : ROW_STEP, :].bitcast(I32),
+                in_=scale_rows[FIRST_ROW + rows * quad : FIRST_ROW + rows * (quad + 1), :].bitcast(I32),
             )
         cast(1, q_raw1)
 
@@ -165,6 +162,6 @@ def tile_attend_pagemean_kernel(tc, qT, k_words, k_scales, offs, out):
 
         result = keep.tile([P, PAGES], F32, name="result")
         nc.vector.scalar_tensor_tensor(
-            out=result[:], in0=total[:], scalar=minus_mean[:], in1=best[:], op0=ALU.mult, op1=ALU.add
+            out=result[:], in0=total[:], scalar=-1.0 / SEG, in1=best[:], op0=ALU.mult, op1=ALU.add
         )
         nc.sync.dma_start(out=out[0], in_=result[:])

@@ -29,7 +29,8 @@ HALF = N // 2
 GROUP = 128
 GROUPS = N // GROUP
 PIECE = 2 * GROUP
-SCALAR_FIRST = 4
+SCALAR_FIRST = 2
+SCALAR_GROUPS = 6
 FLOPS = 2 * NQ * N * PASSES * P * PACK
 
 
@@ -136,6 +137,15 @@ def tile_attend_pagemean_kernel(tc, qT, k_words, k_scales, offs, out):
         pairs = keep.tile([P, N], U32, name="pairs", align_bytes=64)
         gather(0, pairs[:, 0:HALF])
         gather(1, pairs[:, HALF:N])
+        nc.tensor.matmul_mx(
+            out=banks[GROUPS - 1][:],
+            lhsT=q_codes[0][:].bitcast(FP8X4),
+            lhsT_scale=q_planes[0][:],
+            rhs=pairs[:, 0 : HALF // 2].bitcast(FP4X4),
+            rhs_scale=scale_rows[:, 0:HALF],
+            start=True,
+            stop=True,
+        )
         for o in range(PASSES):
             codes = keep.tile([P, 2 * PIECE], U8, name="first%d" % o, align_bytes=64)
             nc.vector.tensor_copy(codes[:].bitcast(U16), halves(pairs[:, 0:PIECE])[:, o, :])
@@ -153,11 +163,13 @@ def tile_attend_pagemean_kernel(tc, qT, k_words, k_scales, offs, out):
                     multiply(o, (piece * PIECE + at) // GROUP, later[:, piece - 1, o, 2 * at : 2 * (at + GROUP)])
         for g in range(SCALAR_FIRST):
             sum_on_scalar(g)
-        for g in range(GROUPS):
+        turns = [g for pair in zip(range(SCALAR_FIRST), range(SCALAR_FIRST, 2 * SCALAR_FIRST)) for g in pair]
+        for g in turns + list(range(2 * SCALAR_FIRST, GROUPS)):
             reduce_on_vector(g, best, ALU.max)
-            if SCALAR_FIRST <= g < GROUPS - 1:
+            if g >= SCALAR_GROUPS:
+                reduce_on_vector(g, total, ALU.add)
+            elif g >= SCALAR_FIRST:
                 sum_on_scalar(g)
-        reduce_on_vector(GROUPS - 1, total, ALU.add)
 
 
         result = keep.tile([P, PAGES], F32, name="result")

@@ -44,7 +44,7 @@ def tile_attend_pagemean_kernel(tc, qT, k_words, k_scales, offs, out):
         scale_pool = keep.tile([P, T], U8, name="scale_pool", align_bytes=64)
 
         def load_queries(o):
-            raw = keep.tile([P, PACK, NQ], F32, name="q_raw%d" % o, tag="raw", align_bytes=64)
+            raw = keep.tile([P, PACK, NQ], F32, name="q_raw%d" % o, tag="raw%d" % o, align_bytes=64)
             rows = qT[0, o * P * PACK : (o + 1) * P * PACK, :]
             nc.sync.dma_start(out=raw[:], in_=rows.rearrange("(p t) q -> p t q", t=PACK))
             return raw
@@ -60,6 +60,7 @@ def tile_attend_pagemean_kernel(tc, qT, k_words, k_scales, offs, out):
             out=word_pool[:].bitcast(I32),
             in_=k_words[0].rearrange("p t b -> p (t b)").bitcast(I32),
         )
+        q_raw1 = load_queries(1)
 
         nc.vector.memset(scale_pool[0:FIRST_ROW, :].bitcast(I32), 0)
 
@@ -123,15 +124,17 @@ def tile_attend_pagemean_kernel(tc, qT, k_words, k_scales, offs, out):
                 )
 
         cast(0, q_raw0)
-        q_raw1 = load_queries(1)
         nc.vector.tensor_copy(scale_rows[:], scale_pool[:].indirect(offsets[:]))
         quantize(0)
         rows = PACK * PASSES
-        for quad in (0, 2, 1, 3):
-            nc.scalar.dma_start(
-                out=k_planes[QUAD * quad : QUAD * quad + PACK, :, :].bitcast(I32),
-                in_=scale_rows[FIRST_ROW + rows * quad : FIRST_ROW + rows * (quad + 1), :].bitcast(I32),
-            )
+        for first in range(0, N, HALF):
+            for quad in (0, 2, 1, 3):
+                nc.sync.dma_start(
+                    out=k_planes[QUAD * quad : QUAD * quad + PACK, :, first : first + HALF].bitcast(I32),
+                    in_=scale_rows[
+                        FIRST_ROW + rows * quad : FIRST_ROW + rows * (quad + 1), first : first + HALF
+                    ].bitcast(I32),
+                )
         cast(1, q_raw1)
 
         pairs = keep.tile([P, N], U32, name="pairs", align_bytes=64)
@@ -153,7 +156,7 @@ def tile_attend_pagemean_kernel(tc, qT, k_words, k_scales, offs, out):
                 quantize(1)
             for g in range(PIECE // GROUP):
                 multiply(o, g, codes[:, 2 * g * GROUP : 2 * (g + 1) * GROUP])
-        later = keep.tile([P, N // PIECE - 1, PASSES, 2 * PIECE], U8, name="later", tag="raw", align_bytes=64)
+        later = keep.tile([P, N // PIECE - 1, PASSES, 2 * PIECE], U8, name="later", tag="raw1", align_bytes=64)
         for piece in range(1, N // PIECE):
             nc.vector.tensor_copy(
                 later[:, piece - 1].bitcast(U16), halves(pairs[:, piece * PIECE : (piece + 1) * PIECE])

@@ -140,15 +140,6 @@ def tile_attend_pagemean_kernel(tc, qT, k_words, k_scales, offs, out):
         pairs = keep.tile([P, N], U32, name="pairs", align_bytes=64)
         gather(0, pairs[:, 0:HALF])
         gather(1, pairs[:, HALF:N])
-        nc.tensor.matmul_mx(
-            out=banks[GROUPS - 1][:],
-            lhsT=q_codes[0][:].bitcast(FP8X4),
-            lhsT_scale=q_planes[0][:],
-            rhs=pairs[:, 0 : HALF // 2].bitcast(FP4X4),
-            rhs_scale=scale_rows[:, 0:HALF],
-            start=True,
-            stop=True,
-        )
         for o in range(PASSES):
             codes = keep.tile([P, 2 * PIECE], U8, name="first%d" % o, align_bytes=64)
             nc.vector.tensor_copy(codes[:].bitcast(U16), halves(pairs[:, 0:PIECE])[:, o, :])

@@ -140,24 +140,34 @@ def tile_attend_pagemean_kernel(tc, qT, k_words, k_scales, offs, out):
         pairs = keep.tile([P, N], U32, name="pairs", align_bytes=64)
         gather(0, pairs[:, 0:HALF])
         gather(1, pairs[:, HALF:N])
-        for o in range(PASSES):
-            codes = keep.tile([P, 2 * PIECE], U8, name="first%d" % o, align_bytes=64)
-            nc.vector.tensor_copy(codes[:].bitcast(U16), halves(pairs[:, 0:PIECE])[:, o, :])
-            if o == 1:
-                quantize(1)
-            for g in range(PIECE // GROUP):
-                multiply(o, g, codes[:, 2 * g * GROUP : 2 * (g + 1) * GROUP])
-        later = keep.tile([P, N // PIECE - 1, PASSES, 2 * PIECE], U8, name="later", tag="raw1", align_bytes=64)
-        for piece in range(1, N // PIECE):
-            nc.vector.tensor_copy(
-                later[:, piece - 1].bitcast(U16), halves(pairs[:, piece * PIECE : (piece + 1) * PIECE])
-            )
+
+        def piece_of(first):
+            return halves(pairs[:, first : first + PIECE])
+
+        def multiply_piece(o, first, codes):
+            for at in range(0, PIECE, GROUP):
+                multiply(o, (first + at) // GROUP, codes[:, 2 * at : 2 * (at + GROUP)])
+
+        for first in range(0, HALF, PIECE):
+            codes = keep.tile([P, 2 * PIECE], U8, name="pass0_%d" % first, align_bytes=64)
+            nc.vector.tensor_copy(codes[:].bitcast(U16), piece_of(first)[:, 0, :])
+            multiply_piece(0, first, codes)
+        codes = keep.tile([P, 2 * PIECE], U8, name="pass1_0", align_bytes=64)
+        nc.vector.tensor_copy(codes[:].bitcast(U16), piece_of(0)[:, 1, :])
+        quantize(1)
+        multiply_piece(1, 0, codes)
+        later = keep.tile([P, 1 + PASSES * HALF // PIECE, 2 * PIECE], U8, name="later", tag="raw1", align_bytes=64)
+        nc.vector.tensor_copy(later[:, 0].bitcast(U16), piece_of(PIECE)[:, 1, :])
+        multiply_piece(1, PIECE, later[:, 0])
+        for first in range(HALF, N, PIECE):
+            row = 1 + PASSES * (first - HALF) // PIECE
+            nc.vector.tensor_copy(later[:, row : row + PASSES].bitcast(U16), piece_of(first))
             for at in range(0, PIECE, GROUP):
                 for o in range(PASSES):
-                    multiply(o, (piece * PIECE + at) // GROUP, later[:, piece - 1, o, 2 * at : 2 * (at + GROUP)])
+                    multiply(o, (first + at) // GROUP, later[:, row + o, 2 * at : 2 * (at + GROUP)])
         for g in range(SCALAR_FIRST):
             sum_on_scalar(g)
-        turns = [g for pair in zip(range(SCALAR_FIRST), range(SCALAR_FIRST, 2 * SCALAR_FIRST)) for g in pair]
+        turns = [g for pair in zip(range(SCALAR_FIRST, 2 * SCALAR_FIRST), range(SCALAR_FIRST)) for g in pair]
         for g in turns + list(range(2 * SCALAR_FIRST, GROUPS)):
             reduce_on_vector(g, best, ALU.max)
             if g >= SCALAR_GROUPS:

@@ -41,10 +41,10 @@ def tile_attend_pagemean_kernel(tc, qT, k_words, k_scales, offs, out):
         psum = ctx.enter_context(tc.psum_pool(name="psum", bufs=1))
 
         offsets = keep.tile([P, N // 16], U16, name="offsets")
-        scale_pool = keep.tile([P, T], U8, name="scale_pool", align_bytes=64)
+        scale_pool = keep.tile([P, T], U8, name="scale_pool", tag="pool", align_bytes=64)
 
-        def load_queries(o):
-            raw = keep.tile([P, PACK, NQ], F32, name="q_raw%d" % o, tag="raw%d" % o, align_bytes=64)
+        def load_queries(o, tag):
+            raw = keep.tile([P, PACK, NQ], F32, name="q_raw%d" % o, tag=tag, align_bytes=64)
             rows = qT[0, o * P * PACK : (o + 1) * P * PACK, :]
             nc.sync.dma_start(out=raw[:], in_=rows.rearrange("(p t) q -> p t q", t=PACK))
             return raw
@@ -55,12 +55,11 @@ def tile_attend_pagemean_kernel(tc, qT, k_words, k_scales, offs, out):
             in_=k_scales.rearrange("o f t -> f o t").bitcast(I32),
         )
         nc.sync.dma_start(offsets[:], offs)
-        q_raw0 = load_queries(0)
         nc.sync.dma_start(
             out=word_pool[:].bitcast(I32),
             in_=k_words[0].rearrange("p t b -> p (t b)").bitcast(I32),
         )
-        q_raw1 = load_queries(1)
+        q_raw0 = load_queries(0, "raw0")
 
         nc.vector.memset(scale_pool[0:FIRST_ROW, :].bitcast(I32), 0)
 
@@ -123,18 +122,29 @@ def tile_attend_pagemean_kernel(tc, qT, k_words, k_scales, offs, out):
                     accum_out=total[:, page : page + 1],
                 )
 
-        cast(0, q_raw0)
-        nc.vector.tensor_copy(scale_rows[:], scale_pool[:].indirect(offsets[:]))
-        quantize(0)
         rows = PACK * PASSES
-        for first in range(0, N, HALF):
+
+        def gather_scales(first):
+            nc.vector.tensor_copy(
+                scale_rows[:, first : first + HALF],
+                scale_pool[:].indirect(offsets[:, first // 16 : (first + HALF) // 16]),
+            )
+
+        def move_scales(queue, first):
             for quad in (0, 2, 1, 3):
-                nc.sync.dma_start(
+                queue.dma_start(
                     out=k_planes[QUAD * quad : QUAD * quad + PACK, :, first : first + HALF].bitcast(I32),
                     in_=scale_rows[
                         FIRST_ROW + rows * quad : FIRST_ROW + rows * (quad + 1), first : first + HALF
                     ].bitcast(I32),
                 )
+
+        gather_scales(0)
+        move_scales(nc.scalar, 0)
+        gather_scales(HALF)
+        q_raw1 = load_queries(1, "pool")
+        move_scales(nc.sync, HALF)
+        cast(0, q_raw0)
         cast(1, q_raw1)
 
         pairs = keep.tile([P, N], U32, name="pairs", align_bytes=64)
@@ -148,15 +158,17 @@ def tile_attend_pagemean_kernel(tc, qT, k_words, k_scales, offs, out):
             for at in range(0, PIECE, GROUP):
                 multiply(o, (first + at) // GROUP, codes[:, 2 * at : 2 * (at + GROUP)])
 
-        for first in range(0, HALF, PIECE):
-            codes = keep.tile([P, 2 * PIECE], U8, name="pass0_%d" % first, align_bytes=64)
-            nc.vector.tensor_copy(codes[:].bitcast(U16), piece_of(first)[:, 0, :])
-            multiply_piece(0, first, codes)
-        codes = keep.tile([P, 2 * PIECE], U8, name="pass1_0", align_bytes=64)
-        nc.vector.tensor_copy(codes[:].bitcast(U16), piece_of(0)[:, 1, :])
+        codes = keep.tile([P, 2 * PIECE], U8, name="pass0_0", align_bytes=64)
+        nc.vector.tensor_copy(codes[:].bitcast(U16), piece_of(0)[:, 0, :])
+        quantize(0)
+        multiply_piece(0, 0, codes)
+        middle = keep.tile([P, 2, 2 * PIECE], U8, name="middle", tag="raw0", align_bytes=64)
+        nc.vector.tensor_copy(middle[:, 0].bitcast(U16), piece_of(PIECE)[:, 0, :])
+        multiply_piece(0, PIECE, middle[:, 0])
+        nc.vector.tensor_copy(middle[:, 1].bitcast(U16), piece_of(0)[:, 1, :])
         quantize(1)
-        multiply_piece(1, 0, codes)
-        later = keep.tile([P, 1 + PASSES * HALF // PIECE, 2 * PIECE], U8, name="later", tag="raw1", align_bytes=64)
+        multiply_piece(1, 0, middle[:, 1])
+        later = keep.tile([P, 1 + PASSES * HALF // PIECE, 2 * PIECE], U8, name="later", tag="pool", align_bytes=64)
         nc.vector.tensor_copy(later[:, 0].bitcast(U16), piece_of(PIECE)[:, 1, :])
         multiply_piece(1, PIECE, later[:, 0])
         for first in range(HALF, N, PIECE):

@@ -29,7 +29,6 @@ HALF = N // 2
 GROUP = 128
 GROUPS = N // GROUP
 PIECE = 2 * GROUP
-SCALAR_FIRST = 2
 SCALAR_GROUPS = 6
 FLOPS = 2 * NQ * N * PASSES * P * PACK
 
@@ -41,7 +40,7 @@ def tile_attend_pagemean_kernel(tc, qT, k_words, k_scales, offs, out):
         psum = ctx.enter_context(tc.psum_pool(name="psum", bufs=1))
 
         offsets = keep.tile([P, N // 16], U16, name="offsets")
-        scale_pool = keep.tile([P, T], U8, name="scale_pool", tag="pool", align_bytes=64)
+        scale_pool = keep.tile([P, T], U8, name="scale_pool", align_bytes=64)
 
         def load_queries(o, tag):
             raw = keep.tile([P, PACK, NQ], F32, name="q_raw%d" % o, tag=tag, align_bytes=64)
@@ -60,6 +59,7 @@ def tile_attend_pagemean_kernel(tc, qT, k_words, k_scales, offs, out):
             in_=k_words[0].rearrange("p t b -> p (t b)").bitcast(I32),
         )
         q_raw0 = load_queries(0, "raw0")
+        q_raw1 = load_queries(1, "raw1")
 
         nc.vector.memset(scale_pool[0:FIRST_ROW, :].bitcast(I32), 0)
 
@@ -124,14 +124,8 @@ def tile_attend_pagemean_kernel(tc, qT, k_words, k_scales, offs, out):
 
         rows = PACK * PASSES
 
-        def gather_scales(first):
-            nc.vector.tensor_copy(
-                scale_rows[:, first : first + HALF],
-                scale_pool[:].indirect(offsets[:, first // 16 : (first + HALF) // 16]),
-            )
-
-        def move_scales(queue, first):
-            for quad in (0, 2, 1, 3):
+        def move_scales(queue, quads, first):
+            for quad in quads:
                 queue.dma_start(
                     out=k_planes[QUAD * quad : QUAD * quad + PACK, :, first : first + HALF].bitcast(I32),
                     in_=scale_rows[
@@ -139,11 +133,17 @@ def tile_attend_pagemean_kernel(tc, qT, k_words, k_scales, offs, out):
                     ].bitcast(I32),
                 )
 
+        def gather_scales(first):
+            nc.vector.tensor_copy(
+                scale_rows[:, first : first + HALF],
+                scale_pool[:].indirect(offsets[:, first // 16 : (first + HALF) // 16]),
+            )
+
         gather_scales(0)
-        move_scales(nc.scalar, 0)
+        move_scales(nc.scalar, (0, 2), 0)
+        move_scales(nc.sync, (1, 3), 0)
         gather_scales(HALF)
-        q_raw1 = load_queries(1, "pool")
-        move_scales(nc.sync, HALF)
+        move_scales(nc.sync, (0, 2, 1, 3), HALF)
         cast(0, q_raw0)
         cast(1, q_raw1)
 
@@ -168,7 +168,7 @@ def tile_attend_pagemean_kernel(tc, qT, k_words, k_scales, offs, out):
         nc.vector.tensor_copy(middle[:, 1].bitcast(U16), piece_of(0)[:, 1, :])
         quantize(1)
         multiply_piece(1, 0, middle[:, 1])
-        later = keep.tile([P, 1 + PASSES * HALF // PIECE, 2 * PIECE], U8, name="later", tag="pool", align_bytes=64)
+        later = keep.tile([P, 1 + PASSES * HALF // PIECE, 2 * PIECE], U8, name="later", tag="raw1", align_bytes=64)
         nc.vector.tensor_copy(later[:, 0].bitcast(U16), piece_of(PIECE)[:, 1, :])
         multiply_piece(1, PIECE, later[:, 0])
         for first in range(HALF, N, PIECE):
@@ -177,16 +177,18 @@ def tile_attend_pagemean_kernel(tc, qT, k_words, k_scales, offs, out):
             for at in range(0, PIECE, GROUP):
                 for o in range(PASSES):
                     multiply(o, (first + at) // GROUP, later[:, row + o, 2 * at : 2 * (at + GROUP)])
-        for g in range(SCALAR_FIRST):
+        scalar_first = range(1, GROUPS // 2, 2)
+        vector_first = range(0, GROUPS // 2, 2)
+        later_banks = range(GROUPS // 2, GROUPS)
+        for g in scalar_first:
             sum_on_scalar(g)
-        turns = [g for pair in zip(range(SCALAR_FIRST, 2 * SCALAR_FIRST), range(SCALAR_FIRST)) for g in pair]
-        for g in turns + list(range(2 * SCALAR_FIRST, GROUPS)):
+        turns = [g for pair in zip(later_banks, scalar_first) for g in pair]
+        for g in list(vector_first) + turns + list(later_banks[len(scalar_first) :]):
             reduce_on_vector(g, best, ALU.max)
             if g >= SCALAR_GROUPS:
                 reduce_on_vector(g, total, ALU.add)
-            elif g >= SCALAR_FIRST:
+            elif g not in scalar_first:
                 sum_on_scalar(g)
-
 
         result = keep.tile([P, PAGES], F32, name="result")
         nc.vector.scalar_tensor_tensor(

@@ -37,13 +37,14 @@ def tile_attend_pagemean_kernel(tc, qT, k_words, k_scales, offs, out):
     nc = tc.nc
     with ExitStack() as ctx:
         keep = ctx.enter_context(tc.tile_pool(name="keep", bufs=1))
+        reuse = [ctx.enter_context(tc.tile_pool(name="reuse%d" % o, bufs=1)) for o in range(PASSES)]
         psum = ctx.enter_context(tc.psum_pool(name="psum", bufs=1))
 
         offsets = keep.tile([P, N // 16], U16, name="offsets")
-        scale_pool = keep.tile([P, T], U8, name="scale_pool", align_bytes=64)
+        scale_pool = reuse[1].tile([P, T], U8, name="scale_pool", align_bytes=64, offset=0)
 
-        def load_queries(o, tag):
-            raw = keep.tile([P, PACK, NQ], F32, name="q_raw%d" % o, tag=tag, align_bytes=64)
+        def load_queries(o):
+            raw = reuse[o].tile([P, PACK, NQ], F32, name="q_raw%d" % o, align_bytes=64, offset=0)
             rows = qT[0, o * P * PACK : (o + 1) * P * PACK, :]
             nc.sync.dma_start(out=raw[:], in_=rows.rearrange("(p t) q -> p t q", t=PACK))
             return raw
@@ -58,8 +59,7 @@ def tile_attend_pagemean_kernel(tc, qT, k_words, k_scales, offs, out):
             out=word_pool[:].bitcast(I32),
             in_=k_words[0].rearrange("p t b -> p (t b)").bitcast(I32),
         )
-        q_raw0 = load_queries(0, "raw0")
-        q_raw1 = load_queries(1, "raw1")
+        q_raw0 = load_queries(0)
 
         nc.vector.memset(scale_pool[0:FIRST_ROW, :].bitcast(I32), 0)
 
@@ -76,10 +76,10 @@ def tile_attend_pagemean_kernel(tc, qT, k_words, k_scales, offs, out):
         banks = [psum.tile([P, HALF], F32, name="bank%d" % b) for b in range(GROUPS)]
         scores = [bank[:, 0:GROUP] for bank in banks]
 
-        def cast(o, raw):
-            nc.scalar.copy(
-                out=q_bf[o][:].rearrange("p (c i) t -> p c t i", i=PACK),
-                in_=raw[:].rearrange("p t (c i) -> p c t i", i=PACK),
+        def cast(copy, o, raw, first, last):
+            copy(
+                out=q_bf[o][:, first:last, :].rearrange("p (c i) t -> p c t i", i=PACK),
+                in_=raw[:, :, first:last].rearrange("p t (c i) -> p c t i", i=PACK),
             )
 
         def quantize(o):
@@ -89,8 +89,7 @@ def tile_attend_pagemean_kernel(tc, qT, k_words, k_scales, offs, out):
                 in_=q_bf[o][:].rearrange("p q t -> p (q t)"),
             )
 
-        def gather(h, pairs):
-            a, b = h * HALF, (h + 1) * HALF
+        def gather(a, b, pairs):
             nc.vector.tensor_copy(pairs, word_pool[:].indirect(offsets[:, a // 16 : b // 16]))
 
         def halves(pairs):
@@ -140,43 +139,50 @@ def tile_attend_pagemean_kernel(tc, qT, k_words, k_scales, offs, out):
             )
 
         gather_scales(0)
-        move_scales(nc.scalar, (0, 2), 0)
-        move_scales(nc.sync, (1, 3), 0)
+        move_scales(nc.scalar, (0, 2, 1, 3), 0)
         gather_scales(HALF)
+        q_raw1 = load_queries(1)
         move_scales(nc.sync, (0, 2, 1, 3), HALF)
-        cast(0, q_raw0)
-        cast(1, q_raw1)
+        cast(nc.scalar.copy, 0, q_raw0, 0, NQ // 2)
+        cast(nc.scalar.copy, 1, q_raw1, 0, NQ // 2)
 
-        pairs = keep.tile([P, N], U32, name="pairs", align_bytes=64)
-        gather(0, pairs[:, 0:HALF])
-        gather(1, pairs[:, HALF:N])
-
-        def piece_of(first):
-            return halves(pairs[:, first : first + PIECE])
+        def part(o, pairs, codes):
+            nc.vector.tensor_copy(codes.bitcast(U16), halves(pairs)[:, o, :])
 
         def multiply_piece(o, first, codes):
             for at in range(0, PIECE, GROUP):
                 multiply(o, (first + at) // GROUP, codes[:, 2 * at : 2 * (at + GROUP)])
 
-        codes = keep.tile([P, 2 * PIECE], U8, name="pass0_0", align_bytes=64)
-        nc.vector.tensor_copy(codes[:].bitcast(U16), piece_of(0)[:, 0, :])
-        quantize(0)
-        multiply_piece(0, 0, codes)
-        middle = keep.tile([P, 2, 2 * PIECE], U8, name="middle", tag="raw0", align_bytes=64)
-        nc.vector.tensor_copy(middle[:, 0].bitcast(U16), piece_of(PIECE)[:, 0, :])
-        multiply_piece(0, PIECE, middle[:, 0])
-        nc.vector.tensor_copy(middle[:, 1].bitcast(U16), piece_of(0)[:, 1, :])
-        quantize(1)
-        multiply_piece(1, 0, middle[:, 1])
-        later = keep.tile([P, 1 + PASSES * HALF // PIECE, 2 * PIECE], U8, name="later", tag="raw1", align_bytes=64)
-        nc.vector.tensor_copy(later[:, 0].bitcast(U16), piece_of(PIECE)[:, 1, :])
-        multiply_piece(1, PIECE, later[:, 0])
-        for first in range(HALF, N, PIECE):
-            row = 1 + PASSES * (first - HALF) // PIECE
-            nc.vector.tensor_copy(later[:, row : row + PASSES].bitcast(U16), piece_of(first))
+        def part_and_multiply(first, pairs):
             for at in range(0, PIECE, GROUP):
+                codes = keep.tile([P, PASSES, 2 * GROUP], U8, name="codes%d" % (first + at), align_bytes=64)
+                nc.vector.tensor_copy(codes[:].bitcast(U16), halves(pairs[:, at : at + GROUP]))
                 for o in range(PASSES):
-                    multiply(o, (first + at) // GROUP, later[:, row + o, 2 * at : 2 * (at + GROUP)])
+                    multiply(o, (first + at) // GROUP, codes[:, o])
+
+        pairs = keep.tile([P, HALF], U32, name="pairs", align_bytes=64)
+        early = [keep.tile([P, 2 * PIECE], U8, name="early%d" % k, align_bytes=64) for k in range(3)]
+        third = reuse[0].tile([P, PIECE], U32, name="third", align_bytes=64, offset=0)
+        fourth = reuse[1].tile([P, PIECE], U32, name="fourth", align_bytes=64, offset=0)
+        later = reuse[1].tile([P, 2 * PIECE], U8, name="later", align_bytes=64, offset=4 * PIECE)
+        gather(0, HALF, pairs[:])
+        cast(nc.vector.tensor_copy, 0, q_raw0, NQ // 2, NQ)
+        part(0, pairs[:, 0:PIECE], early[0][:])
+        part(0, pairs[:, PIECE:HALF], early[1][:])
+        quantize(0)
+        multiply_piece(0, 0, early[0])
+        multiply_piece(0, PIECE, early[1])
+        part(1, pairs[:, 0:PIECE], early[2][:])
+        cast(nc.vector.tensor_copy, 1, q_raw1, NQ // 2, NQ)
+        gather(HALF, HALF + PIECE, third[:])
+        quantize(1)
+        multiply_piece(1, 0, early[2])
+        part(1, pairs[:, PIECE:HALF], later[:])
+        multiply_piece(1, PIECE, later)
+        gather(HALF + PIECE, N, fourth[:])
+        part_and_multiply(HALF, third)
+        part_and_multiply(HALF + PIECE, fourth)
+
         scalar_first = range(1, GROUPS // 2, 2)
         vector_first = range(0, GROUPS // 2, 2)
         later_banks = range(GROUPS // 2, GROUPS)

@@ -26,10 +26,17 @@ NQ = 128
 SEG = 64
 PAGES = N // SEG
 HALF = N // 2
+QUARTER = N // 4
+FIRST_GATHER = N - QUARTER
 GROUP = 128
 GROUPS = N // GROUP
-PIECE = 2 * GROUP
+SCALAR_QUERIES = NQ // 2
+SCALAR_FIRST = 2
 SCALAR_GROUPS = 6
+ALIGN = 64
+PAIRS_BYTES = 4 * QUARTER
+CODES_BYTES = 2 * QUARTER
+RAW_AT = PAIRS_BYTES - ALIGN
 FLOPS = 2 * NQ * N * PASSES * P * PACK
 
 
@@ -40,16 +47,15 @@ def tile_attend_pagemean_kernel(tc, qT, k_words, k_scales, offs, out):
         reuse = [ctx.enter_context(tc.tile_pool(name="reuse%d" % o, bufs=1)) for o in range(PASSES)]
         psum = ctx.enter_context(tc.psum_pool(name="psum", bufs=1))
 
-        offsets = keep.tile([P, N // 16], U16, name="offsets")
-        scale_pool = reuse[1].tile([P, T], U8, name="scale_pool", align_bytes=64, offset=0)
-
         def load_queries(o):
-            raw = reuse[o].tile([P, PACK, NQ], F32, name="q_raw%d" % o, align_bytes=64, offset=0)
+            raw = reuse[o].tile([P, PACK, NQ], F32, name="q_raw%d" % o, align_bytes=ALIGN, offset=RAW_AT)
             rows = qT[0, o * P * PACK : (o + 1) * P * PACK, :]
             nc.sync.dma_start(out=raw[:], in_=rows.rearrange("(p t) q -> p t q", t=PACK))
             return raw
 
-        word_pool = keep.tile([P, T], U32, name="word_pool", align_bytes=64)
+        offsets = keep.tile([P, N // 16], U16, name="offsets")
+        scale_pool = reuse[1].tile([P, T], U8, name="scale_pool", align_bytes=ALIGN, offset=0)
+        word_pool = keep.tile([P, T], U32, name="word_pool", align_bytes=ALIGN)
         nc.sync.dma_start(
             out=scale_pool[FIRST_ROW:P, :].bitcast(I32),
             in_=k_scales.rearrange("o f t -> f o t").bitcast(I32),
@@ -62,19 +68,37 @@ def tile_attend_pagemean_kernel(tc, qT, k_words, k_scales, offs, out):
         q_raw0 = load_queries(0)
 
         nc.vector.memset(scale_pool[0:FIRST_ROW, :].bitcast(I32), 0)
-
-        scale_rows = keep.tile([P, N], U8, name="scale_rows", align_bytes=64)
-        k_planes = keep.tile([P, PASSES, N], U8, name="k_planes", align_bytes=64)
+        scale_rows = keep.tile([P, N], U8, name="scale_rows", align_bytes=ALIGN)
+        k_planes = keep.tile([P, PASSES, N], U8, name="k_planes", align_bytes=ALIGN)
         nc.vector.memset(k_planes[:].bitcast(I32), 0)
 
-        q_bf = [keep.tile([P, NQ, PACK], BF16, name="q_bf%d" % o, align_bytes=64) for o in range(PASSES)]
-        q_codes = [keep.tile([P, NQ], U32, name="q_codes%d" % o, align_bytes=64) for o in range(PASSES)]
-        q_planes = [keep.tile([P, NQ], U8, name="q_plane%d" % o, align_bytes=64) for o in range(PASSES)]
+        q_bf = [
+            keep.tile([P, NQ, PACK], BF16, name="q_bf0", align_bytes=ALIGN),
+            reuse[0].tile([P, NQ, PACK], BF16, name="q_bf1", align_bytes=ALIGN, offset=0),
+        ]
+        q_codes = [keep.tile([P, NQ], U32, name="q_codes%d" % o, align_bytes=ALIGN) for o in range(PASSES)]
+        q_planes = [keep.tile([P, NQ], U8, name="q_plane%d" % o, align_bytes=ALIGN) for o in range(PASSES)]
         best = keep.tile([P, PAGES], F32, name="best")
         total = keep.tile([P, PAGES], F32, name="total")
         spill = keep.tile([P, PAGES, SEG], F32, name="spill")
         banks = [psum.tile([P, HALF], F32, name="bank%d" % b) for b in range(GROUPS)]
         scores = [bank[:, 0:GROUP] for bank in banks]
+
+        def listed(pool, first, last):
+            return pool[:].indirect(offsets[:, first // 16 : last // 16])
+
+        def gather_scales(first):
+            nc.vector.tensor_copy(scale_rows[:, first : first + HALF], listed(scale_pool, first, first + HALF))
+
+        def move_scales(queue, first):
+            rows = PACK * PASSES
+            for quad in (0, 2, 1, 3):
+                queue.dma_start(
+                    out=k_planes[QUAD * quad : QUAD * quad + PACK, :, first : first + HALF].bitcast(I32),
+                    in_=scale_rows[
+                        FIRST_ROW + rows * quad : FIRST_ROW + rows * (quad + 1), first : first + HALF
+                    ].bitcast(I32),
+                )
 
         def cast(copy, o, raw, first, last):
             copy(
@@ -89,22 +113,23 @@ def tile_attend_pagemean_kernel(tc, qT, k_words, k_scales, offs, out):
                 in_=q_bf[o][:].rearrange("p q t -> p (q t)"),
             )
 
-        def gather(a, b, pairs):
-            nc.vector.tensor_copy(pairs, word_pool[:].indirect(offsets[:, a // 16 : b // 16]))
-
         def halves(pairs):
             return pairs.bitcast(U16).rearrange("p (n o) -> p o n", o=PASSES)
 
-        def multiply(o, g, words):
-            nc.tensor.matmul_mx(
-                out=scores[g],
-                lhsT=q_codes[o][:].bitcast(FP8X4),
-                lhsT_scale=q_planes[o][:],
-                rhs=words.bitcast(FP4X4),
-                rhs_scale=k_planes[:, o, g * GROUP : (g + 1) * GROUP],
-                start=(o == 0),
-                stop=(o == PASSES - 1),
-            )
+        def part(o, pairs, codes):
+            nc.vector.tensor_copy(codes.bitcast(U16), halves(pairs)[:, o, :])
+
+        def multiply(o, first, last, codes):
+            for at in range(first, last, GROUP):
+                nc.tensor.matmul_mx(
+                    out=scores[at // GROUP],
+                    lhsT=q_codes[o][:].bitcast(FP8X4),
+                    lhsT_scale=q_planes[o][:],
+                    rhs=codes[:, 2 * (at - first) : 2 * (at - first + GROUP)].bitcast(FP4X4),
+                    rhs_scale=k_planes[:, o, at : at + GROUP],
+                    start=(o == 0),
+                    stop=(o == PASSES - 1),
+                )
 
         def reduce_on_vector(g, into, op):
             pages = scores[g].rearrange("p (j i) -> p j i", i=SEG)
@@ -121,79 +146,52 @@ def tile_attend_pagemean_kernel(tc, qT, k_words, k_scales, offs, out):
                     accum_out=total[:, page : page + 1],
                 )
 
-        rows = PACK * PASSES
-
-        def move_scales(queue, quads, first):
-            for quad in quads:
-                queue.dma_start(
-                    out=k_planes[QUAD * quad : QUAD * quad + PACK, :, first : first + HALF].bitcast(I32),
-                    in_=scale_rows[
-                        FIRST_ROW + rows * quad : FIRST_ROW + rows * (quad + 1), first : first + HALF
-                    ].bitcast(I32),
-                )
-
-        def gather_scales(first):
-            nc.vector.tensor_copy(
-                scale_rows[:, first : first + HALF],
-                scale_pool[:].indirect(offsets[:, first // 16 : (first + HALF) // 16]),
-            )
-
         gather_scales(0)
-        move_scales(nc.scalar, (0, 2, 1, 3), 0)
+        move_scales(nc.scalar, 0)
         gather_scales(HALF)
         q_raw1 = load_queries(1)
-        move_scales(nc.sync, (0, 2, 1, 3), HALF)
-        cast(nc.scalar.copy, 0, q_raw0, 0, NQ // 2)
-        cast(nc.scalar.copy, 1, q_raw1, 0, NQ // 2)
+        move_scales(nc.sync, HALF)
+        cast(nc.scalar.copy, 0, q_raw0, 0, SCALAR_QUERIES)
+        cast(nc.scalar.copy, 1, q_raw1, 0, SCALAR_QUERIES)
 
-        def part(o, pairs, codes):
-            nc.vector.tensor_copy(codes.bitcast(U16), halves(pairs)[:, o, :])
+        def behind_cast(o, shape, name, k):
+            return reuse[o].tile(shape, U8, name=name, align_bytes=ALIGN, offset=PAIRS_BYTES + k * CODES_BYTES)
 
-        def multiply_piece(o, first, codes):
-            for at in range(0, PIECE, GROUP):
-                multiply(o, (first + at) // GROUP, codes[:, 2 * at : 2 * (at + GROUP)])
+        pairs = keep.tile([P, FIRST_GATHER], U32, name="pairs", align_bytes=ALIGN)
+        last_pairs = reuse[1].tile([P, QUARTER], U32, name="last_pairs", align_bytes=ALIGN, offset=0)
+        pass0 = keep.tile([P, 2 * HALF], U8, name="pass0", align_bytes=ALIGN)
+        pass1 = behind_cast(0, [P, 2 * CODES_BYTES], "pass1", 0)
 
-        def part_and_multiply(first, pairs):
-            for at in range(0, PIECE, GROUP):
-                codes = keep.tile([P, PASSES, 2 * GROUP], U8, name="codes%d" % (first + at), align_bytes=64)
-                nc.vector.tensor_copy(codes[:].bitcast(U16), halves(pairs[:, at : at + GROUP]))
-                for o in range(PASSES):
-                    multiply(o, (first + at) // GROUP, codes[:, o])
+        def score_group(first, words):
+            codes = behind_cast(1, [P, PASSES, 2 * GROUP], "both%d" % first, (first - HALF) // GROUP)
+            nc.vector.tensor_copy(codes[:].bitcast(U16), halves(words))
+            for o in range(PASSES):
+                multiply(o, first, first + GROUP, codes[:, o])
 
-        pairs = keep.tile([P, HALF], U32, name="pairs", align_bytes=64)
-        early = [keep.tile([P, 2 * PIECE], U8, name="early%d" % k, align_bytes=64) for k in range(3)]
-        third = reuse[0].tile([P, PIECE], U32, name="third", align_bytes=64, offset=0)
-        fourth = reuse[1].tile([P, PIECE], U32, name="fourth", align_bytes=64, offset=0)
-        later = reuse[1].tile([P, 2 * PIECE], U8, name="later", align_bytes=64, offset=4 * PIECE)
-        gather(0, HALF, pairs[:])
-        cast(nc.vector.tensor_copy, 0, q_raw0, NQ // 2, NQ)
-        part(0, pairs[:, 0:PIECE], early[0][:])
-        part(0, pairs[:, PIECE:HALF], early[1][:])
+        nc.vector.tensor_copy(pairs[:], listed(word_pool, 0, FIRST_GATHER))
+        cast(nc.vector.tensor_copy, 0, q_raw0, SCALAR_QUERIES, NQ)
+        part(0, pairs[:, 0:HALF], pass0[:])
         quantize(0)
-        multiply_piece(0, 0, early[0])
-        multiply_piece(0, PIECE, early[1])
-        part(1, pairs[:, 0:PIECE], early[2][:])
-        cast(nc.vector.tensor_copy, 1, q_raw1, NQ // 2, NQ)
-        gather(HALF, HALF + PIECE, third[:])
+        multiply(0, 0, HALF, pass0)
+        cast(nc.vector.tensor_copy, 1, q_raw1, SCALAR_QUERIES, NQ)
+        part(1, pairs[:, 0:HALF], pass1[:])
         quantize(1)
-        multiply_piece(1, 0, early[2])
-        part(1, pairs[:, PIECE:HALF], later[:])
-        multiply_piece(1, PIECE, later)
-        gather(HALF + PIECE, N, fourth[:])
-        part_and_multiply(HALF, third)
-        part_and_multiply(HALF + PIECE, fourth)
+        multiply(1, 0, HALF, pass1)
+        score_group(HALF, pairs[:, HALF : HALF + GROUP])
+        nc.vector.tensor_copy(last_pairs[:], listed(word_pool, FIRST_GATHER, N))
+        score_group(HALF + GROUP, pairs[:, HALF + GROUP : FIRST_GATHER])
+        for at in range(0, QUARTER, GROUP):
+            score_group(FIRST_GATHER + at, last_pairs[:, at : at + GROUP])
 
-        scalar_first = range(1, GROUPS // 2, 2)
-        vector_first = range(0, GROUPS // 2, 2)
-        later_banks = range(GROUPS // 2, GROUPS)
-        for g in scalar_first:
+        for g in range(SCALAR_FIRST):
             sum_on_scalar(g)
-        turns = [g for pair in zip(later_banks, scalar_first) for g in pair]
-        for g in list(vector_first) + turns + list(later_banks[len(scalar_first) :]):
+        pairs_of_banks = zip(range(SCALAR_FIRST), range(2 * SCALAR_FIRST, 3 * SCALAR_FIRST))
+        turns = [g for pair in pairs_of_banks for g in pair]
+        for g in list(range(SCALAR_FIRST, 2 * SCALAR_FIRST)) + turns + list(range(3 * SCALAR_FIRST, GROUPS)):
             reduce_on_vector(g, best, ALU.max)
             if g >= SCALAR_GROUPS:
                 reduce_on_vector(g, total, ALU.add)
-            elif g not in scalar_first:
+            elif g >= SCALAR_FIRST:
                 sum_on_scalar(g)
 
         result = keep.tile([P, PAGES], F32, name="result")

@@ -31,7 +31,6 @@ FIRST_GATHER = N - QUARTER
 GROUP = 128
 GROUPS = N // GROUP
 SCALAR_QUERIES = NQ // 2
-SCALAR_FIRST = 2
 SCALAR_GROUPS = 6
 ALIGN = 64
 PAIRS_BYTES = 4 * QUARTER
@@ -183,15 +182,17 @@ def tile_attend_pagemean_kernel(tc, qT, k_words, k_scales, offs, out):
         for at in range(0, QUARTER, GROUP):
             score_group(FIRST_GATHER + at, last_pairs[:, at : at + GROUP])
 
-        for g in range(SCALAR_FIRST):
+        scalar_first = range(1, GROUPS // 2, 2)
+        vector_first = range(0, GROUPS // 2, 2)
+        later_banks = range(GROUPS // 2, GROUPS)
+        for g in scalar_first:
             sum_on_scalar(g)
-        pairs_of_banks = zip(range(SCALAR_FIRST), range(2 * SCALAR_FIRST, 3 * SCALAR_FIRST))
-        turns = [g for pair in pairs_of_banks for g in pair]
-        for g in list(range(SCALAR_FIRST, 2 * SCALAR_FIRST)) + turns + list(range(3 * SCALAR_FIRST, GROUPS)):
+        turns = [g for pair in zip(later_banks, scalar_first) for g in pair]
+        for g in list(vector_first) + turns + list(later_banks[len(scalar_first) :]):
             reduce_on_vector(g, best, ALU.max)
             if g >= SCALAR_GROUPS:
                 reduce_on_vector(g, total, ALU.add)
-            elif g >= SCALAR_FIRST:
+            elif g not in scalar_first:
                 sum_on_scalar(g)
 
         result = keep.tile([P, PAGES], F32, name="result")

@@ -27,15 +27,17 @@ SEG = 64
 PAGES = N // SEG
 HALF = N // 2
 QUARTER = N // 4
-FIRST_GATHER = N - QUARTER
 GROUP = 128
 GROUPS = N // GROUP
-SCALAR_QUERIES = NQ // 2
+SCALAR_QUERIES = (96, 80)
 SCALAR_GROUPS = 6
 ALIGN = 64
 PAIRS_BYTES = 4 * QUARTER
 CODES_BYTES = 2 * QUARTER
 RAW_AT = PAIRS_BYTES - ALIGN
+PARTED_BYTES = 2 * HALF
+FIRST_PIECE = 32
+RAW_BYTES = 4 * PACK * NQ
 FLOPS = 2 * NQ * N * PASSES * P * PACK
 
 
@@ -43,17 +45,16 @@ def tile_attend_pagemean_kernel(tc, qT, k_words, k_scales, offs, out):
     nc = tc.nc
     with ExitStack() as ctx:
         keep = ctx.enter_context(tc.tile_pool(name="keep", bufs=1))
-        reuse = [ctx.enter_context(tc.tile_pool(name="reuse%d" % o, bufs=1)) for o in range(PASSES)]
+        parted = ctx.enter_context(tc.tile_pool(name="parted", bufs=1))
+        reuse = ctx.enter_context(tc.tile_pool(name="reuse", bufs=1))
         psum = ctx.enter_context(tc.psum_pool(name="psum", bufs=1))
 
-        def load_queries(o):
-            raw = reuse[o].tile([P, PACK, NQ], F32, name="q_raw%d" % o, align_bytes=ALIGN, offset=RAW_AT)
+        def load_queries(o, raw):
             rows = qT[0, o * P * PACK : (o + 1) * P * PACK, :]
-            nc.sync.dma_start(out=raw[:], in_=rows.rearrange("(p t) q -> p t q", t=PACK))
-            return raw
+            nc.sync.dma_start(out=raw, in_=rows.rearrange("(p t) q -> p t q", t=PACK))
 
         offsets = keep.tile([P, N // 16], U16, name="offsets")
-        scale_pool = reuse[1].tile([P, T], U8, name="scale_pool", align_bytes=ALIGN, offset=0)
+        scale_pool = reuse.tile([P, T], U8, name="scale_pool", align_bytes=ALIGN, offset=0)
         word_pool = keep.tile([P, T], U32, name="word_pool", align_bytes=ALIGN)
         nc.sync.dma_start(
             out=scale_pool[FIRST_ROW:P, :].bitcast(I32),
@@ -64,7 +65,9 @@ def tile_attend_pagemean_kernel(tc, qT, k_words, k_scales, offs, out):
             out=word_pool[:].bitcast(I32),
             in_=k_words[0].rearrange("p t b -> p (t b)").bitcast(I32),
         )
-        q_raw0 = load_queries(0)
+        shared = keep.tile([P, RAW_AT + RAW_BYTES], U8, name="shared", align_bytes=ALIGN)
+        q_raw0 = shared[:, RAW_AT:].bitcast(F32).rearrange("p (t q) -> p t q", t=PACK)
+        load_queries(0, q_raw0)
 
         nc.vector.memset(scale_pool[0:FIRST_ROW, :].bitcast(I32), 0)
         scale_rows = keep.tile([P, N], U8, name="scale_rows", align_bytes=ALIGN)
@@ -72,8 +75,8 @@ def tile_attend_pagemean_kernel(tc, qT, k_words, k_scales, offs, out):
         nc.vector.memset(k_planes[:].bitcast(I32), 0)
 
         q_bf = [
-            keep.tile([P, NQ, PACK], BF16, name="q_bf0", align_bytes=ALIGN),
-            reuse[0].tile([P, NQ, PACK], BF16, name="q_bf1", align_bytes=ALIGN, offset=0),
+            keep.tile([P, NQ, PACK], BF16, name="q_bf0", align_bytes=ALIGN)[:],
+            shared[:, 0 : RAW_BYTES // 2].bitcast(BF16).rearrange("p (q t) -> p q t", t=PACK),
         ]
         q_codes = [keep.tile([P, NQ], U32, name="q_codes%d" % o, align_bytes=ALIGN) for o in range(PASSES)]
         q_planes = [keep.tile([P, NQ], U8, name="q_plane%d" % o, align_bytes=ALIGN) for o in range(PASSES)]
@@ -109,7 +112,7 @@ def tile_attend_pagemean_kernel(tc, qT, k_words, k_scales, offs, out):
             nc.vector.quantize_mx(
                 out=q_codes[o][:].bitcast(FP8X4),
                 scales=q_planes[o][:],
-                in_=q_bf[o][:].rearrange("p q t -> p (q t)"),
+                in_=q_bf[o].rearrange("p q t -> p (q t)"),
             )
 
         def halves(pairs):
@@ -148,39 +151,54 @@ def tile_attend_pagemean_kernel(tc, qT, k_words, k_scales, offs, out):
         gather_scales(0)
         move_scales(nc.scalar, 0)
         gather_scales(HALF)
-        q_raw1 = load_queries(1)
+        q_raw1 = reuse.tile([P, PACK, NQ], F32, name="q_raw1", align_bytes=ALIGN, offset=RAW_AT)
+        load_queries(1, q_raw1[:])
         move_scales(nc.sync, HALF)
-        cast(nc.scalar.copy, 0, q_raw0, 0, SCALAR_QUERIES)
-        cast(nc.scalar.copy, 1, q_raw1, 0, SCALAR_QUERIES)
 
-        def behind_cast(o, shape, name, k):
-            return reuse[o].tile(shape, U8, name=name, align_bytes=ALIGN, offset=PAIRS_BYTES + k * CODES_BYTES)
+        def cast_on_scalar(o, raw):
+            one = parted.tile([P, 1], F32, name="one%d" % o, align_bytes=ALIGN, offset=o * PARTED_BYTES)
+            nc.vector.memset(one[:], 1.0)
 
-        pairs = keep.tile([P, FIRST_GATHER], U32, name="pairs", align_bytes=ALIGN)
-        last_pairs = reuse[1].tile([P, QUARTER], U32, name="last_pairs", align_bytes=ALIGN, offset=0)
-        pass0 = keep.tile([P, 2 * HALF], U8, name="pass0", align_bytes=ALIGN)
-        pass1 = behind_cast(0, [P, 2 * CODES_BYTES], "pass1", 0)
+            def scaled(out, in_):
+                nc.scalar.activation(out=out, in_=in_, func=ACT.Copy, scale=one[:])
+
+            cut = SCALAR_QUERIES[o] - FIRST_PIECE
+            cast(scaled, o, raw, cut, SCALAR_QUERIES[o])
+            cast(nc.scalar.copy, o, raw, 0, cut)
+
+        cast_on_scalar(0, q_raw0)
+        cast_on_scalar(1, q_raw1)
+
+        pairs = keep.tile([P, HALF], U32, name="pairs", align_bytes=ALIGN)
+        third_pairs = keep.tile([P, QUARTER], U32, name="third_pairs", align_bytes=ALIGN)
+        last_pairs = reuse.tile([P, QUARTER], U32, name="last_pairs", align_bytes=ALIGN, offset=0)
+        pass0, pass1 = [
+            parted.tile([P, PARTED_BYTES], U8, name="pass%d" % o, align_bytes=ALIGN, offset=o * PARTED_BYTES)
+            for o in range(PASSES)
+        ]
 
         def score_group(first, words):
-            codes = behind_cast(1, [P, PASSES, 2 * GROUP], "both%d" % first, (first - HALF) // GROUP)
+            at = PAIRS_BYTES + (first - HALF) // GROUP * CODES_BYTES
+            codes = reuse.tile([P, PASSES, 2 * GROUP], U8, name="both%d" % first, align_bytes=ALIGN, offset=at)
             nc.vector.tensor_copy(codes[:].bitcast(U16), halves(words))
             for o in range(PASSES):
                 multiply(o, first, first + GROUP, codes[:, o])
 
-        nc.vector.tensor_copy(pairs[:], listed(word_pool, 0, FIRST_GATHER))
-        cast(nc.vector.tensor_copy, 0, q_raw0, SCALAR_QUERIES, NQ)
-        part(0, pairs[:, 0:HALF], pass0[:])
+        nc.vector.tensor_copy(pairs[:], listed(word_pool, 0, HALF))
+        nc.vector.tensor_copy(third_pairs[:], listed(word_pool, HALF, HALF + QUARTER))
+        cast(nc.vector.tensor_copy, 0, q_raw0, SCALAR_QUERIES[0], NQ)
+        part(0, pairs[:], pass0[:])
         quantize(0)
         multiply(0, 0, HALF, pass0)
-        cast(nc.vector.tensor_copy, 1, q_raw1, SCALAR_QUERIES, NQ)
-        part(1, pairs[:, 0:HALF], pass1[:])
+        cast(nc.vector.tensor_copy, 1, q_raw1, SCALAR_QUERIES[1], NQ)
+        part(1, pairs[:], pass1[:])
         quantize(1)
         multiply(1, 0, HALF, pass1)
-        score_group(HALF, pairs[:, HALF : HALF + GROUP])
-        nc.vector.tensor_copy(last_pairs[:], listed(word_pool, FIRST_GATHER, N))
-        score_group(HALF + GROUP, pairs[:, HALF + GROUP : FIRST_GATHER])
+        score_group(HALF, third_pairs[:, 0:GROUP])
+        nc.vector.tensor_copy(last_pairs[:], listed(word_pool, HALF + QUARTER, N))
+        score_group(HALF + GROUP, third_pairs[:, GROUP:QUARTER])
         for at in range(0, QUARTER, GROUP):
-            score_group(FIRST_GATHER + at, last_pairs[:, at : at + GROUP])
+            score_group(HALF + QUARTER + at, last_pairs[:, at : at + GROUP])
 
         scalar_first = range(1, GROUPS // 2, 2)
         vector_first = range(0, GROUPS // 2, 2)

from contextlib import ExitStack

import concourse.mybir as mybir

F32 = mybir.dt.float32
BF16 = mybir.dt.bfloat16
I32 = mybir.dt.int32
U32 = mybir.dt.uint32
U16 = mybir.dt.uint16
U8 = mybir.dt.uint8
FP8X4 = mybir.dt.float8_e4m3fn_x4
FP4X4 = mybir.dt.float4_e2m1fn_x4
ALU = mybir.AluOpType
AX = mybir.AxisListType
ACT = mybir.ActivationFunctionType

P = 128
QUAD = 32
PACK = 4
PASSES = 2
SCALE_ROWS = 32
FIRST_ROW = P - SCALE_ROWS
T = 4096
N = 1024
NQ = 128
SEG = 64
PAGES = N // SEG
HALF = N // 2
QUARTER = N // 4
GROUP = 128
GROUPS = N // GROUP
SCALAR_QUERIES = (96, 80)
SCALAR_GROUPS = 6
ALIGN = 64
PAIRS_BYTES = 4 * QUARTER
CODES_BYTES = 2 * QUARTER
RAW_AT = PAIRS_BYTES - ALIGN
PARTED_BYTES = 2 * HALF
FIRST_PIECE = 32
RAW_BYTES = 4 * PACK * NQ
FLOPS = 2 * NQ * N * PASSES * P * PACK


def tile_attend_pagemean_kernel(tc, qT, k_words, k_scales, offs, out):
    nc = tc.nc
    with ExitStack() as ctx:
        keep = ctx.enter_context(tc.tile_pool(name="keep", bufs=1))
        parted = ctx.enter_context(tc.tile_pool(name="parted", bufs=1))
        reuse = ctx.enter_context(tc.tile_pool(name="reuse", bufs=1))
        psum = ctx.enter_context(tc.psum_pool(name="psum", bufs=1))

        def load_queries(o, raw):
            rows = qT[0, o * P * PACK : (o + 1) * P * PACK, :]
            nc.sync.dma_start(out=raw, in_=rows.rearrange("(p t) q -> p t q", t=PACK))

        offsets = keep.tile([P, N // 16], U16, name="offsets")
        scale_pool = reuse.tile([P, T], U8, name="scale_pool", align_bytes=ALIGN, offset=0)
        word_pool = keep.tile([P, T], U32, name="word_pool", align_bytes=ALIGN)
        nc.sync.dma_start(
            out=scale_pool[FIRST_ROW:P, :].bitcast(I32),
            in_=k_scales.rearrange("o f t -> f o t").bitcast(I32),
        )
        nc.sync.dma_start(offsets[:], offs)
        nc.sync.dma_start(
            out=word_pool[:].bitcast(I32),
            in_=k_words[0].rearrange("p t b -> p (t b)").bitcast(I32),
        )
        shared = keep.tile([P, RAW_AT + RAW_BYTES], U8, name="shared", align_bytes=ALIGN)
        q_raw0 = shared[:, RAW_AT:].bitcast(F32).rearrange("p (t q) -> p t q", t=PACK)
        load_queries(0, q_raw0)

        nc.vector.memset(scale_pool[0:FIRST_ROW, :].bitcast(I32), 0)
        scale_rows = keep.tile([P, N], U8, name="scale_rows", align_bytes=ALIGN)
        k_planes = keep.tile([P, PASSES, N], U8, name="k_planes", align_bytes=ALIGN)
        nc.vector.memset(k_planes[:].bitcast(I32), 0)

        q_bf = [
            keep.tile([P, NQ, PACK], BF16, name="q_bf0", align_bytes=ALIGN)[:],
            shared[:, 0 : RAW_BYTES // 2].bitcast(BF16).rearrange("p (q t) -> p q t", t=PACK),
        ]
        q_codes = [keep.tile([P, NQ], U32, name="q_codes%d" % o, align_bytes=ALIGN) for o in range(PASSES)]
        q_planes = [keep.tile([P, NQ], U8, name="q_plane%d" % o, align_bytes=ALIGN) for o in range(PASSES)]
        best = keep.tile([P, PAGES], F32, name="best")
        total = keep.tile([P, PAGES], F32, name="total")
        spill = keep.tile([P, PAGES, SEG], F32, name="spill")
        banks = [psum.tile([P, HALF], F32, name="bank%d" % b) for b in range(GROUPS)]
        scores = [bank[:, 0:GROUP] for bank in banks]

        def listed(pool, first, last):
            return pool[:].indirect(offsets[:, first // 16 : last // 16])

        def gather_scales(first):
            nc.vector.tensor_copy(scale_rows[:, first : first + HALF], listed(scale_pool, first, first + HALF))

        def move_scales(queue, first):
            rows = PACK * PASSES
            for quad in (0, 2, 1, 3):
                queue.dma_start(
                    out=k_planes[QUAD * quad : QUAD * quad + PACK, :, first : first + HALF].bitcast(I32),
                    in_=scale_rows[
                        FIRST_ROW + rows * quad : FIRST_ROW + rows * (quad + 1), first : first + HALF
                    ].bitcast(I32),
                )

        def cast(copy, o, raw, first, last):
            copy(
                out=q_bf[o][:, first:last, :].rearrange("p (c i) t -> p c t i", i=PACK),
                in_=raw[:, :, first:last].rearrange("p t (c i) -> p c t i", i=PACK),
            )

        def quantize(o):
            nc.vector.quantize_mx(
                out=q_codes[o][:].bitcast(FP8X4),
                scales=q_planes[o][:],
                in_=q_bf[o].rearrange("p q t -> p (q t)"),
            )

        def halves(pairs):
            return pairs.bitcast(U16).rearrange("p (n o) -> p o n", o=PASSES)

        def part(o, pairs, codes):
            nc.vector.tensor_copy(codes.bitcast(U16), halves(pairs)[:, o, :])

        def multiply(o, first, last, codes):
            for at in range(first, last, GROUP):
                nc.tensor.matmul_mx(
                    out=scores[at // GROUP],
                    lhsT=q_codes[o][:].bitcast(FP8X4),
                    lhsT_scale=q_planes[o][:],
                    rhs=codes[:, 2 * (at - first) : 2 * (at - first + GROUP)].bitcast(FP4X4),
                    rhs_scale=k_planes[:, o, at : at + GROUP],
                    start=(o == 0),
                    stop=(o == PASSES - 1),
                )

        def reduce_on_vector(g, into, op):
            pages = scores[g].rearrange("p (j i) -> p j i", i=SEG)
            first = g * GROUP // SEG
            nc.vector.tensor_reduce(out=into[:, first : first + GROUP // SEG], in_=pages, axis=AX.X, op=op)

        def sum_on_scalar(g):
            for c in range(0, GROUP, SEG):
                page = (g * GROUP + c) // SEG
                nc.scalar.activation(
                    out=spill[:, page, :],
                    in_=scores[g][:, c : c + SEG],
                    func=ACT.Copy,
                    accum_out=total[:, page : page + 1],
                )

        gather_scales(0)
        move_scales(nc.scalar, 0)
        gather_scales(HALF)
        q_raw1 = reuse.tile([P, PACK, NQ], F32, name="q_raw1", align_bytes=ALIGN, offset=RAW_AT)
        load_queries(1, q_raw1[:])
        move_scales(nc.sync, HALF)

        def cast_on_scalar(o, raw):
            one = parted.tile([P, 1], F32, name="one%d" % o, align_bytes=ALIGN, offset=o * PARTED_BYTES)
            nc.vector.memset(one[:], 1.0)

            def scaled(out, in_):
                nc.scalar.activation(out=out, in_=in_, func=ACT.Copy, scale=one[:])

            cut = SCALAR_QUERIES[o] - FIRST_PIECE
            cast(scaled, o, raw, cut, SCALAR_QUERIES[o])
            cast(nc.scalar.copy, o, raw, 0, cut)

        cast_on_scalar(0, q_raw0)
        cast_on_scalar(1, q_raw1)

        pairs = keep.tile([P, HALF], U32, name="pairs", align_bytes=ALIGN)
        third_pairs = keep.tile([P, QUARTER], U32, name="third_pairs", align_bytes=ALIGN)
        last_pairs = reuse.tile([P, QUARTER], U32, name="last_pairs", align_bytes=ALIGN, offset=0)
        pass0, pass1 = [
            parted.tile([P, PARTED_BYTES], U8, name="pass%d" % o, align_bytes=ALIGN, offset=o * PARTED_BYTES)
            for o in range(PASSES)
        ]

        def score_group(first, words):
            at = PAIRS_BYTES + (first - HALF) // GROUP * CODES_BYTES
            codes = reuse.tile([P, PASSES, 2 * GROUP], U8, name="both%d" % first, align_bytes=ALIGN, offset=at)
            nc.vector.tensor_copy(codes[:].bitcast(U16), halves(words))
            for o in range(PASSES):
                multiply(o, first, first + GROUP, codes[:, o])

        nc.vector.tensor_copy(pairs[:], listed(word_pool, 0, HALF))
        nc.vector.tensor_copy(third_pairs[:], listed(word_pool, HALF, HALF + QUARTER))
        cast(nc.vector.tensor_copy, 0, q_raw0, SCALAR_QUERIES[0], NQ)
        part(0, pairs[:], pass0[:])
        quantize(0)
        multiply(0, 0, HALF, pass0)
        cast(nc.vector.tensor_copy, 1, q_raw1, SCALAR_QUERIES[1], NQ)
        part(1, pairs[:], pass1[:])
        quantize(1)
        multiply(1, 0, HALF, pass1)
        score_group(HALF, third_pairs[:, 0:GROUP])
        nc.vector.tensor_copy(last_pairs[:], listed(word_pool, HALF + QUARTER, N))
        score_group(HALF + GROUP, third_pairs[:, GROUP:QUARTER])
        for at in range(0, QUARTER, GROUP):
            score_group(HALF + QUARTER + at, last_pairs[:, at : at + GROUP])

        scalar_first = range(1, GROUPS // 2, 2)
        vector_first = range(0, GROUPS // 2, 2)
        later_banks = range(GROUPS // 2, GROUPS)
        for g in scalar_first:
            sum_on_scalar(g)
        turns = [g for pair in zip(later_banks, scalar_first) for g in pair]
        for g in list(vector_first) + turns + list(later_banks[len(scalar_first) :]):
            reduce_on_vector(g, best, ALU.max)
            if g >= SCALAR_GROUPS:
                reduce_on_vector(g, total, ALU.add)
            elif g not in scalar_first:
                sum_on_scalar(g)

        result = keep.tile([P, PAGES], F32, name="result")
        nc.vector.scalar_tensor_tensor(
            out=result[:], in0=total[:], scalar=-1.0 / SEG, in1=best[:], op0=ALU.mult, op1=ALU.add
        )
        nc.sync.dma_start(out=out[0], in_=result[:])
